import numpy as np
import ml_dtypes


def mxq(x, axis, fmt="e4m3"):
    dtype, down = {"e4m3": (ml_dtypes.float8_e4m3fn, 7), "e5m2": (ml_dtypes.float8_e5m2, 14)}[fmt]
    v = np.moveaxis(np.asarray(x, np.float32).astype(ml_dtypes.bfloat16).astype(np.float64), axis, -1)
    blocks = v.reshape(v.shape[:-1] + (-1, 32))
    amax = np.abs(blocks).max(-1, keepdims=True)
    byte = np.maximum(np.where(amax > 0, np.frexp(amax)[1] - 1 + 127, 0) - down, 1)
    scale = np.exp2(byte - 127.0)
    codes = (blocks / scale).astype(np.float32).astype(dtype).astype(np.float64)
    return np.moveaxis((codes * scale).reshape(v.shape), -1, axis)


WIDE = False


def mx_kscale(k):
    if not WIDE:
        return np.ones(k)
    levels = np.array([10, -10, 5, -5, 0])
    if k % 512:
        return np.exp2(np.random.permutation(np.resize(levels, k // 32))).repeat(32)
    a = np.empty((k // 512, 16))
    for p in range(k // 512):
        a[p, :8] = np.random.permutation(np.resize(levels, 8))
        for g in range(8):
            far = levels[np.abs(levels - a[p, g]) >= 10]
            a[p, g + 8] = far[np.random.randint(len(far))]
    return np.exp2(a.ravel()).repeat(32)


def f64(x):
    return np.asarray(x).astype(np.float64)


def striped(idx):
    return np.tile(idx.reshape(-1, 16).T, (8, 1)).astype(np.uint16)


def unstriped(offs):
    return offs[:16].T.reshape(-1).astype(np.int64)


E2M1 = np.array([0.0, 0.5, 1.0, 1.5, 2.0, 3.0, 4.0, 6.0, -0.0, -0.5, -1.0, -1.5, -2.0, -3.0, -4.0, -6.0])


def pack_weight(w, fmt):
    k, n = w.shape
    w = f64(np.asarray(w, np.float32).astype(ml_dtypes.bfloat16)).reshape(k // 32, 32, n)
    amax = np.abs(w).max(1)
    if fmt == "e4m3":
        byte = np.frexp(amax)[1] - 1 + 127 - 7
    else:
        mant, ex = np.frexp(amax / 6.0)
        byte = np.where(mant > 0.5, ex, ex - 1) + 127
    byte = np.clip(np.where(amax > 0, byte, 1), 1, 254)
    scaled = (w * np.exp2(127.0 - byte)[:, None, :]).reshape(k, n).astype(np.float32)
    by_word = np.ascontiguousarray(scaled.reshape(k // 512, 128, 4, n).transpose(0, 1, 3, 2))
    if fmt == "e4m3":
        words = by_word.astype(ml_dtypes.float8_e4m3fn).view(np.uint8)
    else:
        c = by_word.astype(ml_dtypes.float4_e2m1fn).view(np.uint8) & 0xF
        words = (c[..., 0::2] | (c[..., 1::2] << 4)).reshape(k // 512, 128, 2 * n)
    return np.ascontiguousarray(words), np.ascontiguousarray(byte.astype(np.uint8).reshape(k // 512, 16, n))


def unpack_weight(words, scales, fmt):
    g, _, n = scales.shape
    words = np.ascontiguousarray(words).reshape(g, 128, n, -1)
    if fmt == "e4m3":
        vals = words.view(ml_dtypes.float8_e4m3fn).astype(np.float64)
    else:
        nib = np.empty((g, 128, n, 4), np.uint8)
        nib[..., 0::2] = words & 0xF
        nib[..., 1::2] = words >> 4
        vals = E2M1[nib]
    vals = vals * np.repeat(np.exp2(scales.astype(np.float64) - 127.0), 8, axis=1)[..., None]
    return vals.transpose(0, 1, 3, 2).reshape(g * 512, n)


def gelu(v):
    return 0.5 * v * (1.0 + np.tanh(np.sqrt(2.0 / np.pi) * (v + 0.044715 * v**3)))


K, T, S, H, N = 1024, 4096, 1024, 512, 512

def setup_inputs():
    n = np.random.standard_normal
    s = mx_kscale(K)[:, None]
    u = mx_kscale(H)[:, None]
    tab_words, tab_scales = pack_weight(n((K, T)) * s, "e4m3")
    we = n((K, H)) / np.sqrt(K) / s * u.T
    ws4_words, ws4_scales = pack_weight(n((K, H)) / np.sqrt(K) / s, "e2m1")
    wi8_words, wi8_scales = pack_weight(n((K, H)) / np.sqrt(K) / s, "e4m3")
    st4_words, st4_scales = pack_weight(n((H, N)) / np.sqrt(H) / u, "e2m1")
    return {"tab_words": tab_words, "tab_scales": tab_scales,
            "offs": striped(np.random.permutation(T)[:S]),
            "offs2": striped(np.random.permutation(T)[:S]),
            "offs3": striped(np.random.permutation(T)[:S]),
            "we": we.astype(np.float32),
            "ws4_words": ws4_words, "ws4_scales": ws4_scales,
            "wi8_words": wi8_words, "wi8_scales": wi8_scales,
            "st4_words": st4_words, "st4_scales": st4_scales,
            "b": (0.5 * n(N)).astype(np.float32)}

def reference(tab_words, tab_scales, offs, offs2, offs3, we, ws4_words, ws4_scales,
              wi8_words, wi8_scales, st4_words, st4_scales, b):
    ve = unpack_weight(tab_words, tab_scales, "e4m3")[:, unstriped(offs)]
    vs = unpack_weight(tab_words, tab_scales, "e4m3")[:, unstriped(offs2)]
    vi = unpack_weight(tab_words, tab_scales, "e4m3")[:, unstriped(offs3)]
    e = mxq(f64(we), 0, "e4m3").T @ ve
    c = unpack_weight(ws4_words, ws4_scales, "e2m1").T @ vs
    i = unpack_weight(wi8_words, wi8_scales, "e4m3").T @ vi
    h = e * c / (1.0 + i * i)
    y = unpack_weight(st4_words, st4_scales, "e2m1").T @ mxq(h, 0, "e4m3")
    return y + f64(b)[:, None]

@@ -1,0 +1,297 @@
+from contextlib import ExitStack
+
+import concourse.mybir as mybir
+from concourse.masks import make_identity
+
+K, T, S, H, N = 1024, 4096, 1024, 512, 512
+FLOPS = 2 * S * (3 * K * H + H * N)
+
+F32 = mybir.dt.float32
+BF16 = mybir.dt.bfloat16
+I32 = mybir.dt.int32
+U32 = mybir.dt.uint32
+U16 = mybir.dt.uint16
+U8 = mybir.dt.uint8
+FP8X4 = mybir.dt.float8_e4m3fn_x4
+FP4X4 = mybir.dt.float4_e2m1fn_x4
+ACT = mybir.ActivationFunctionType
+MULT = mybir.AluOpType.mult
+ADD = mybir.AluOpType.add
+
+P = 128
+PASSES = K // 512
+CHUNK = 512
+BLOCK = 128
+CHUNKS = S // CHUNK
+BLOCKS = S // BLOCK
+PER = CHUNK // BLOCK
+
+
+def tile_list_inhibited_enzyme_fluxes_kernel(
+    tc, tab_words, tab_scales, offs, offs2, offs3, we, ws4_words, ws4_scales,
+    wi8_words, wi8_scales, st4_words, st4_scales, b, out,
+):
+    nc = tc.nc
+    with ExitStack() as ctx:
+        keep = ctx.enter_context(tc.tile_pool(name="keep", bufs=1))
+        ring = ctx.enter_context(tc.tile_pool(name="ring", bufs=4))
+        psum = ctx.enter_context(tc.psum_pool(name="psum", bufs=1))
+
+        lists = {name: keep.tile([P, S // 16], U16, name="list_" + name) for name in "iec"}
+        tab_sc = keep.tile([P, T // 4], I32, align_bytes=64)
+        tab_w = [keep.tile([P, T], I32, name="tab_w%d" % a, align_bytes=64) for a in range(PASSES)]
+        wi_w = keep.tile([P, PASSES, H], I32, align_bytes=64)
+        ws_w = keep.tile([P, PASSES, H // 2], I32, align_bytes=64)
+        st_w = keep.tile([P, N // 2], I32, align_bytes=64)
+        wi_sc = keep.tile([P, PASSES, H // 4], I32, align_bytes=64)
+        ws_sc = keep.tile([P, PASSES, H // 4], I32, align_bytes=64)
+        st_sc = keep.tile([P, N // 4], I32, align_bytes=64)
+        we_raw = [keep.tile([P, 4, H], F32, name="we_raw%d" % a) for a in range(PASSES)]
+        bias = keep.tile([P, N // P], F32)
+        shifted = keep.tile([P, S // 4], I32, align_bytes=64)
+        ident = keep.tile([P, P], F32)
+        warm_in = keep.tile([P, 1], F32)
+        warm_out = keep.tile([P, 1], F32)
+
+        nc.vector.memset(tab_sc[:], 0)
+        nc.vector.memset(warm_in[:], 1.0)
+        nc.scalar.activation(warm_out[:], warm_in[:], ACT.Abs_reciprocal_sqrt)
+        nc.vector.memset(wi_sc[:], 0)
+        nc.vector.memset(ws_sc[:], 0)
+        nc.vector.memset(st_sc[:], 0)
+        nc.vector.memset(shifted[:], 0)
+        make_identity(nc, ident[:])
+
+        nc.sync.dma_start(lists["i"][:], offs3)
+        nc.sync.dma_start(lists["c"][:], offs2)
+        nc.sync.dma_start(lists["e"][:], offs)
+        with nc.allow_non_contiguous_dma(reason="one bias value a partition"):
+            nc.sync.dma_start(bias[:], b.rearrange("(c p) -> p c", p=P))
+        tab_sc_hbm = tab_scales.bitcast(I32)
+        for a in range(PASSES):
+            for r in range(4):
+                nc.sync.dma_start(tab_sc[4 * a + r : P : 32, :], tab_sc_hbm[a, r:16:4, :])
+
+        def load_tab(a):
+            nc.sync.dma_start(tab_w[a][:], tab_words[a].rearrange("p t i -> p (t i)").bitcast(I32))
+
+        def load_planes(tile, scales):
+            hbm = scales.bitcast(I32)
+            for r in range(4):
+                nc.sync.dma_start(tile[r:P:32, :, :], hbm[:, r:16:4, :].rearrange("a q n -> q a n"))
+
+        def load_we(a):
+            nc.sync.dma_start(we_raw[a][:], we[512 * a : 512 * (a + 1), :].rearrange("(p j) r -> p j r", j=4))
+
+        load_tab(0)
+        nc.sync.dma_start(wi_w[:], wi8_words.rearrange("a p y i -> p a (y i)").bitcast(I32))
+        load_planes(wi_sc, wi8_scales)
+        load_tab(1)
+        nc.sync.dma_start(ws_w[:], ws4_words.rearrange("a p y -> p a y").bitcast(I32))
+        load_planes(ws_sc, ws4_scales)
+        load_we(0)
+        load_we(1)
+        nc.sync.dma_start(st_w[:], st4_words[0].bitcast(I32))
+        st_sc_hbm = st4_scales.bitcast(I32)
+        for r in range(4):
+            nc.sync.dma_start(st_sc[r:P:32, :], st_sc_hbm[0, r:16:4, :])
+
+        picked_sc = {name: keep.tile([P, S], U8, name="picked_sc_" + name, align_bytes=64) for name in "iec"}
+        picked_w = {}
+        reuse = {("e", 0, 0): ("i", 0, 0), ("c", 0, 1): ("i", 1, 0), ("e", 0, 1): ("i", 0, 1)}
+
+        def gather_scales(name):
+            nc.vector.tensor_copy(picked_sc[name][:], tab_sc[:].bitcast(U8).indirect(lists[name][:]))
+
+        def gather_words(name, a, ch):
+            cols = slice(ch * CHUNK // 16, (ch + 1) * CHUNK // 16)
+            slot = "picked_w_%s%d%d" % reuse.get((name, a, ch), (name, a, ch))
+            picked_w[name, a, ch] = keep.tile([P, CHUNK], U32, name=slot, tag=slot, align_bytes=64)
+            nc.vector.tensor_copy(picked_w[name, a, ch][:], tab_w[a][:].bitcast(U32).indirect(lists[name][:, cols]))
+
+        we_bf = keep.tile([P, PASSES, H, 4], BF16, align_bytes=64)
+        we_w = keep.tile([P, PASSES, H], U32, align_bytes=64)
+        we_sc = keep.tile([P, PASSES, H], U8, align_bytes=64)
+
+        def round_we(a):
+            nc.gpsimd.tensor_scalar(we_bf[:, a], we_raw[a][:].rearrange("p j r -> p r j"), 1.0, 0.0, MULT, ADD)
+
+        def quantise_we():
+            nc.vector.quantize_mx(out=we_w[:].rearrange("p a r -> p (a r)").bitcast(FP8X4),
+                                  scales=we_sc[:].rearrange("p a r -> p (a r)"),
+                                  in_=we_bf[:].rearrange("p a r j -> p (a r j)"))
+
+        def bank(number, shape):
+            return psum.tile([P] + shape, F32, name="bank%d" % number, tag="bank%d" % number)
+
+        turn_of_drain = [0]
+
+        def drain_bank(shape):
+            turn_of_drain[0] += 1
+            return bank(6 + turn_of_drain[0] % 2, shape)
+
+        sums = {}
+
+        def multiply(name, blk):
+            ch, cols = blk // PER, slice((blk % PER) * BLOCK, (blk % PER + 1) * BLOCK)
+            all_cols = slice(blk * BLOCK, (blk + 1) * BLOCK)
+            if name == "e":
+                acc = bank(4 + blk % 2, [H])
+            elif name == "c" and blk < PER:
+                acc = bank(4 + blk, [H])
+            else:
+                acc = bank(blk % PER, [H])
+            for a in range(PASSES):
+                if name == "c":
+                    plane = picked_sc["c"][:, all_cols] if a == 0 else shifted[:].bitcast(U8)[:, all_cols]
+                    rhs = ws_w[:, a, :].bitcast(U8).bitcast(FP4X4)
+                    rhs_scale = ws_sc[:, a, :].bitcast(U8)
+                else:
+                    plane = picked_sc[name][4 * a :, all_cols]
+                    rhs = (wi_w if name == "i" else we_w)[:, a, :].bitcast(FP8X4)
+                    rhs_scale = wi_sc[:, a, :].bitcast(U8) if name == "i" else we_sc[:, a, :]
+                nc.tensor.matmul_mx(out=acc[:], lhsT=picked_w[name, a, ch][:, cols].bitcast(FP8X4), lhsT_scale=plane,
+                                    rhs=rhs, rhs_scale=rhs_scale, start=(a == 0), stop=(a == PASSES - 1))
+            sums[name, blk] = acc[:].rearrange("p (m u e) -> p u m e", u=2, e=2)
+
+        def as_pairs(tile):
+            return tile[:].rearrange("p (u m e) -> p u m e", u=2, e=2)
+
+        squares = {}
+        damp = {}
+        damped = {}
+        rates = {}
+        grouped = {}
+        h_mx = {}
+
+        def square_inhibitor(blk):
+            squares[blk] = ring.tile([P, H], F32, name="square")
+            nc.scalar.activation(as_pairs(squares[blk]), sums["i", blk], ACT.Square)
+
+        def damping(blk):
+            root = ring.tile([P, H], F32)
+            nc.scalar.activation(root[:], squares[blk][:], ACT.Abs_reciprocal_sqrt, bias=1.0)
+            damp[blk] = ring.tile([P, H], F32, name="damp")
+            if blk in range(PER, BLOCKS):
+                nc.gpsimd.tensor_tensor(damp[blk][:], root[:], root[:], MULT)
+            else:
+                nc.scalar.activation(damp[blk][:], root[:], ACT.Square)
+
+        def damp_substrate(blk):
+            damped[blk] = ring.tile([P, H], F32, name="damped", bufs=BLOCKS)
+            nc.vector.tensor_tensor(as_pairs(damped[blk]), sums["c", blk], as_pairs(damp[blk]), MULT)
+
+        def rate(blk):
+            rates[blk] = ring.tile([P, H], BF16, name="rate", align_bytes=64)
+            nc.vector.tensor_tensor(as_pairs(rates[blk]), sums["e", blk], as_pairs(damped[blk]), MULT)
+
+        def turn(group):
+            turned = drain_bank([len(group), 2, BLOCK])
+            for g, blk in enumerate(group):
+                words = rates[blk][:].bitcast(F32)
+                for u in range(2):
+                    nc.tensor.transpose(turned[:, g, u, :], words[:, u * P : (u + 1) * P], ident[:])
+            grouped[group] = ring.tile([P, len(group), BLOCK, 4], BF16, name="grouped", align_bytes=64)
+            nc.scalar.copy(grouped[group][:].bitcast(F32), turned[:].rearrange("p g u j -> p g j u"))
+
+        def quantise_rates(group):
+            h_w = ring.tile([P, len(group) * BLOCK], U32, align_bytes=64)
+            h_sc = ring.tile([P, len(group) * BLOCK], U8, align_bytes=64)
+            nc.vector.quantize_mx(out=h_w[:].bitcast(FP8X4), scales=h_sc[:],
+                                  in_=grouped[group][:].rearrange("p g j t -> p (g j t)"))
+            h_mx[group] = h_w, h_sc
+
+        def flux(group):
+            h_w, h_sc = h_mx[group]
+            width = len(group) * BLOCK
+            st_bytes = st_w[:].bitcast(U8)
+            st_plane = st_sc[:].bitcast(U8)
+            last = group[-1] == BLOCKS - 1
+            per_bank = 2 if last else H // width
+            for first in range(0, N // P, per_bank):
+                y = drain_bank([per_bank, width])
+                for c in range(first, first + per_bank):
+                    nc.tensor.matmul_mx(out=y[:, c - first, :], lhsT=st_bytes[:, 2 * P * c : 2 * P * (c + 1)].bitcast(FP4X4),
+                                        lhsT_scale=st_plane[:, P * c : P * (c + 1)],
+                                        rhs=h_w[:].bitcast(FP8X4), rhs_scale=h_sc[:], start=True, stop=True)
+                result = ring.tile([P, per_bank, width], F32, bufs=6)
+                for c in range(first, first + per_bank):
+                    if last and first > 0:
+                        nc.vector.tensor_scalar(result[:, c - first, :], y[:, c - first, :], bias[:, c : c + 1], None, ADD)
+                    else:
+                        nc.scalar.activation(result[:, c - first, :], y[:, c - first, :], ACT.Identity, bias=bias[:, c : c + 1])
+                rows = out[first * P : (first + per_bank) * P, group[0] * BLOCK : group[0] * BLOCK + width]
+                nc.sync.dma_start(rows.rearrange("(c p) j -> p c j", p=P), result[:])
+
+        gather_scales("i")
+        gather_scales("c")
+        nc.gpsimd.dma_start(shifted[0 : P - 4, :], picked_sc["c"][4:P, :].bitcast(I32))
+        gather_words("i", 0, 0)
+        gather_scales("e")
+        gather_words("c", 0, 0)
+        gather_words("i", 0, 1)
+        for a in range(PASSES):
+            round_we(a)
+        gather_words("i", 1, 0)
+        gather_words("c", 1, 0)
+        gather_words("i", 1, 1)
+        for blk in range(PER):
+            multiply("i", blk)
+        for blk in range(PER):
+            square_inhibitor(blk)
+            damping(blk)
+        for blk in range(PER):
+            multiply("c", blk)
+        for blk in range(PER, BLOCKS):
+            multiply("i", blk)
+            square_inhibitor(blk)
+        for blk in range(PER, BLOCKS):
+            damping(blk)
+        gather_words("e", 0, 0)
+        gather_words("e", 1, 0)
+        damp_substrate(0)
+        damp_substrate(1)
+        gather_words("c", 0, 1)
+        damp_substrate(2)
+        damp_substrate(3)
+        quantise_we()
+        gather_words("c", 1, 1)
+        multiply("e", 0)
+        multiply("e", 1)
+        rate(0)
+        gather_words("e", 0, 1)
+        rate(1)
+        multiply("e", 2)
+        multiply("e", 3)
+        turn((0, 1))
+        for blk in range(PER, BLOCKS):
+            multiply("c", blk)
+        rate(2)
+        gather_words("e", 1, 1)
+        rate(3)
+        quantise_rates((0, 1))
+        turn((2, 3))
+        multiply("e", 4)
+        multiply("e", 5)
+        flux((0, 1))
+        damp_substrate(4)
+        damp_substrate(5)
+        quantise_rates((2, 3))
+        rate(4)
+        rate(5)
+        multiply("e", 6)
+        multiply("e", 7)
+        turn((4, 5))
+        flux((2, 3))
+        damp_substrate(6)
+        damp_substrate(7)
+        rate(6)
+        quantise_rates((4, 5))
+        rate(7)
+        turn((6,))
+        turn((7,))
+        flux((4, 5))
+        quantise_rates((6,))
+        quantise_rates((7,))
+        flux((6,))
+        flux((7,))

@@ -34,7 +34,7 @@ def tile_list_inhibited_enzyme_fluxes_kernel(
     nc = tc.nc
     with ExitStack() as ctx:
         keep = ctx.enter_context(tc.tile_pool(name="keep", bufs=1))
-        ring = ctx.enter_context(tc.tile_pool(name="ring", bufs=4))
+        ring = ctx.enter_context(tc.tile_pool(name="ring", bufs=6))
         psum = ctx.enter_context(tc.psum_pool(name="psum", bufs=1))
 
         lists = {name: keep.tile([P, S // 16], U16, name="list_" + name) for name in "iec"}
@@ -84,13 +84,13 @@ def tile_list_inhibited_enzyme_fluxes_kernel(
             nc.sync.dma_start(we_raw[a][:], we[512 * a : 512 * (a + 1), :].rearrange("(p j) r -> p j r", j=4))
 
         load_tab(0)
+        load_tab(1)
+        load_we(0)
         nc.sync.dma_start(wi_w[:], wi8_words.rearrange("a p y i -> p a (y i)").bitcast(I32))
         load_planes(wi_sc, wi8_scales)
-        load_tab(1)
+        load_we(1)
         nc.sync.dma_start(ws_w[:], ws4_words.rearrange("a p y -> p a y").bitcast(I32))
         load_planes(ws_sc, ws4_scales)
-        load_we(0)
-        load_we(1)
         nc.sync.dma_start(st_w[:], st4_words[0].bitcast(I32))
         st_sc_hbm = st4_scales.bitcast(I32)
         for r in range(4):
@@ -98,7 +98,7 @@ def tile_list_inhibited_enzyme_fluxes_kernel(
 
         picked_sc = {name: keep.tile([P, S], U8, name="picked_sc_" + name, align_bytes=64) for name in "iec"}
         picked_w = {}
-        reuse = {("e", 0, 0): ("i", 0, 0), ("c", 0, 1): ("i", 1, 0), ("e", 0, 1): ("i", 0, 1)}
+        reuse = {("c", 0, 1): ("i", 0, 0), ("e", 0, 1): ("i", 0, 1), ("c", 1, 1): ("i", 1, 0), ("e", 1, 1): ("i", 1, 1)}
 
         def gather_scales(name):
             nc.vector.tensor_copy(picked_sc[name][:], tab_sc[:].bitcast(U8).indirect(lists[name][:]))
@@ -113,34 +113,27 @@ def tile_list_inhibited_enzyme_fluxes_kernel(
         we_w = keep.tile([P, PASSES, H], U32, align_bytes=64)
         we_sc = keep.tile([P, PASSES, H], U8, align_bytes=64)
 
-        def round_we(a):
-            nc.gpsimd.tensor_scalar(we_bf[:, a], we_raw[a][:].rearrange("p j r -> p r j"), 1.0, 0.0, MULT, ADD)
-
         def quantise_we():
             nc.vector.quantize_mx(out=we_w[:].rearrange("p a r -> p (a r)").bitcast(FP8X4),
                                   scales=we_sc[:].rearrange("p a r -> p (a r)"),
                                   in_=we_bf[:].rearrange("p a r j -> p (a r j)"))
 
-        def bank(number, shape):
-            return psum.tile([P] + shape, F32, name="bank%d" % number, tag="bank%d" % number)
+        free_banks = list(range(8))
+        held = {}
 
-        turn_of_drain = [0]
+        def take_bank(key, shape):
+            held[key] = free_banks.pop(0)
+            return psum.tile([P] + shape, F32, name="bank%d" % held[key], tag="bank%d" % held[key])
 
-        def drain_bank(shape):
-            turn_of_drain[0] += 1
-            return bank(6 + turn_of_drain[0] % 2, shape)
+        def give_bank(key):
+            free_banks.append(held.pop(key))
 
         sums = {}
 
         def multiply(name, blk):
             ch, cols = blk // PER, slice((blk % PER) * BLOCK, (blk % PER + 1) * BLOCK)
             all_cols = slice(blk * BLOCK, (blk + 1) * BLOCK)
-            if name == "e":
-                acc = bank(4 + blk % 2, [H])
-            elif name == "c" and blk < PER:
-                acc = bank(4 + blk, [H])
-            else:
-                acc = bank(blk % PER, [H])
+            acc = take_bank((name, blk), [H])
             for a in range(PASSES):
                 if name == "c":
                     plane = picked_sc["c"][:, all_cols] if a == 0 else shifted[:].bitcast(U8)[:, all_cols]
@@ -165,14 +158,15 @@ def tile_list_inhibited_enzyme_fluxes_kernel(
         h_mx = {}
 
         def square_inhibitor(blk):
-            squares[blk] = ring.tile([P, H], F32, name="square")
+            squares[blk] = ring.tile([P, H], F32, name="square", bufs=BLOCKS)
             nc.scalar.activation(as_pairs(squares[blk]), sums["i", blk], ACT.Square)
+            give_bank(("i", blk))
 
         def damping(blk):
             root = ring.tile([P, H], F32)
             nc.scalar.activation(root[:], squares[blk][:], ACT.Abs_reciprocal_sqrt, bias=1.0)
-            damp[blk] = ring.tile([P, H], F32, name="damp")
-            if blk in range(PER, BLOCKS):
+            damp[blk] = ring.tile([P, H], F32, name="damp", bufs=BLOCKS)
+            if blk in ():
                 nc.gpsimd.tensor_tensor(damp[blk][:], root[:], root[:], MULT)
             else:
                 nc.scalar.activation(damp[blk][:], root[:], ACT.Square)
@@ -180,19 +174,22 @@ def tile_list_inhibited_enzyme_fluxes_kernel(
         def damp_substrate(blk):
             damped[blk] = ring.tile([P, H], F32, name="damped", bufs=BLOCKS)
             nc.vector.tensor_tensor(as_pairs(damped[blk]), sums["c", blk], as_pairs(damp[blk]), MULT)
+            give_bank(("c", blk))
 
         def rate(blk):
             rates[blk] = ring.tile([P, H], BF16, name="rate", align_bytes=64)
             nc.vector.tensor_tensor(as_pairs(rates[blk]), sums["e", blk], as_pairs(damped[blk]), MULT)
+            give_bank(("e", blk))
 
         def turn(group):
-            turned = drain_bank([len(group), 2, BLOCK])
+            turned = take_bank("turned", [len(group), 2, BLOCK])
             for g, blk in enumerate(group):
                 words = rates[blk][:].bitcast(F32)
                 for u in range(2):
                     nc.tensor.transpose(turned[:, g, u, :], words[:, u * P : (u + 1) * P], ident[:])
             grouped[group] = ring.tile([P, len(group), BLOCK, 4], BF16, name="grouped", align_bytes=64)
             nc.scalar.copy(grouped[group][:].bitcast(F32), turned[:].rearrange("p g u j -> p g j u"))
+            give_bank("turned")
 
         def quantise_rates(group):
             h_w = ring.tile([P, len(group) * BLOCK], U32, align_bytes=64)
@@ -206,92 +203,65 @@ def tile_list_inhibited_enzyme_fluxes_kernel(
             width = len(group) * BLOCK
             st_bytes = st_w[:].bitcast(U8)
             st_plane = st_sc[:].bitcast(U8)
-            last = group[-1] == BLOCKS - 1
-            per_bank = 2 if last else H // width
+            shared = group[-1] >= 1
+            per_bank = 2 if shared else H // width
+            result = ring.tile([P, N // P, width], F32, bufs=BLOCKS)
             for first in range(0, N // P, per_bank):
-                y = drain_bank([per_bank, width])
+                y = take_bank("y", [per_bank, width])
                 for c in range(first, first + per_bank):
                     nc.tensor.matmul_mx(out=y[:, c - first, :], lhsT=st_bytes[:, 2 * P * c : 2 * P * (c + 1)].bitcast(FP4X4),
                                         lhsT_scale=st_plane[:, P * c : P * (c + 1)],
                                         rhs=h_w[:].bitcast(FP8X4), rhs_scale=h_sc[:], start=True, stop=True)
-                result = ring.tile([P, per_bank, width], F32, bufs=6)
-                for c in range(first, first + per_bank):
-                    if last and first > 0:
-                        nc.vector.tensor_scalar(result[:, c - first, :], y[:, c - first, :], bias[:, c : c + 1], None, ADD)
-                    else:
-                        nc.scalar.activation(result[:, c - first, :], y[:, c - first, :], ACT.Identity, bias=bias[:, c : c + 1])
-                rows = out[first * P : (first + per_bank) * P, group[0] * BLOCK : group[0] * BLOCK + width]
-                nc.sync.dma_start(rows.rearrange("(c p) j -> p c j", p=P), result[:])
+                if shared and first > 0:
+                    spread = bias[:, first : first + per_bank].unsqueeze(2).to_broadcast([P, per_bank, width])
+                    nc.vector.tensor_tensor(result[:, first : first + per_bank, :], y[:], spread, ADD)
+                else:
+                    for c in range(first, first + per_bank):
+                        nc.scalar.activation(result[:, c, :], y[:, c - first, :], ACT.Identity, bias=bias[:, c : c + 1])
+                give_bank("y")
+            cols = out[:, group[0] * BLOCK : group[0] * BLOCK + width]
+            nc.sync.dma_start(cols.rearrange("(c p) j -> p c j", p=P), result[:])
 
         gather_scales("i")
         gather_scales("c")
         nc.gpsimd.dma_start(shifted[0 : P - 4, :], picked_sc["c"][4:P, :].bitcast(I32))
-        gather_words("i", 0, 0)
         gather_scales("e")
+        gather_words("i", 0, 0)
         gather_words("c", 0, 0)
         gather_words("i", 0, 1)
-        for a in range(PASSES):
-            round_we(a)
-        gather_words("i", 1, 0)
-        gather_words("c", 1, 0)
-        gather_words("i", 1, 1)
-        for blk in range(PER):
-            multiply("i", blk)
-        for blk in range(PER):
-            square_inhibitor(blk)
-            damping(blk)
-        for blk in range(PER):
-            multiply("c", blk)
-        for blk in range(PER, BLOCKS):
-            multiply("i", blk)
-            square_inhibitor(blk)
-        for blk in range(PER, BLOCKS):
-            damping(blk)
         gather_words("e", 0, 0)
+        gather_words("i", 1, 0)
+        gather_words("i", 1, 1)
+        nc.scalar.copy(we_bf[:, 0], we_raw[0][:].rearrange("p j r -> p r j"))
+        for blk in range(BLOCKS):
+            multiply("i", blk)
+            square_inhibitor(blk)
+            if blk < 0:
+                damping(blk)
+        gather_words("c", 1, 0)
         gather_words("e", 1, 0)
-        damp_substrate(0)
-        damp_substrate(1)
-        gather_words("c", 0, 1)
-        damp_substrate(2)
-        damp_substrate(3)
+        nc.vector.tensor_copy(we_bf[:, 1], we_raw[1][:].rearrange("p j r -> p r j"))
         quantise_we()
+        gather_words("c", 0, 1)
         gather_words("c", 1, 1)
-        multiply("e", 0)
-        multiply("e", 1)
-        rate(0)
         gather_words("e", 0, 1)
-        rate(1)
-        multiply("e", 2)
-        multiply("e", 3)
-        turn((0, 1))
-        for blk in range(PER, BLOCKS):
-            multiply("c", blk)
-        rate(2)
         gather_words("e", 1, 1)
-        rate(3)
-        quantise_rates((0, 1))
-        turn((2, 3))
-        multiply("e", 4)
-        multiply("e", 5)
-        flux((0, 1))
-        damp_substrate(4)
-        damp_substrate(5)
-        quantise_rates((2, 3))
-        rate(4)
-        rate(5)
-        multiply("e", 6)
-        multiply("e", 7)
-        turn((4, 5))
-        flux((2, 3))
-        damp_substrate(6)
-        damp_substrate(7)
-        rate(6)
-        quantise_rates((4, 5))
-        rate(7)
-        turn((6,))
-        turn((7,))
-        flux((4, 5))
-        quantise_rates((6,))
-        quantise_rates((7,))
-        flux((6,))
-        flux((7,))
+        groups = {group[-1]: group for group in [(0,),(1,),(2,),(3,),(4,),(5,),(6,),(7,)]}
+        dampings = list(range(0, BLOCKS))
+        for step in range(-6, 2 * BLOCKS):
+            while dampings and dampings[0] <= step + 3:
+                damping(dampings.pop(0))
+            if 0 <= step + 3 < BLOCKS:
+                multiply("c", step + 3)
+            if 0 <= step + 0 < BLOCKS:
+                multiply("e", step + 0)
+            if 0 <= step < BLOCKS:
+                damp_substrate(step)
+            if 0 <= step - 1 < BLOCKS:
+                rate(step - 1)
+            if step - 3 in groups:
+                turn(groups[step - 3])
+            if step - 3 in groups:
+                quantise_rates(groups[step - 3])
+            if step - 5 in groups:
+                flux(groups[step - 5])

@@ -65,11 +65,10 @@ def tile_list_inhibited_enzyme_fluxes_kernel(
         nc.sync.dma_start(lists["i"][:], offs3)
         nc.sync.dma_start(lists["c"][:], offs2)
         nc.sync.dma_start(lists["e"][:], offs)
-        with nc.allow_non_contiguous_dma(reason="one bias value a partition"):
-            nc.sync.dma_start(bias[:], b.rearrange("(c p) -> p c", p=P))
+        nc.sync.dma_start(st_w[:], st4_words[0].bitcast(I32))
         tab_sc_hbm = tab_scales.bitcast(I32)
-        for a in range(PASSES):
-            for r in range(4):
+        for r in range(4):
+            for a in range(PASSES):
                 nc.sync.dma_start(tab_sc[4 * a + r : P : 32, :], tab_sc_hbm[a, r:16:4, :])
 
         def load_tab(a):
@@ -91,14 +90,15 @@ def tile_list_inhibited_enzyme_fluxes_kernel(
         load_we(1)
         nc.sync.dma_start(ws_w[:], ws4_words.rearrange("a p y -> p a y").bitcast(I32))
         load_planes(ws_sc, ws4_scales)
-        nc.sync.dma_start(st_w[:], st4_words[0].bitcast(I32))
+        with nc.allow_non_contiguous_dma(reason="one bias value a partition"):
+            nc.sync.dma_start(bias[:], b.rearrange("(c p) -> p c", p=P))
         st_sc_hbm = st4_scales.bitcast(I32)
         for r in range(4):
             nc.sync.dma_start(st_sc[r:P:32, :], st_sc_hbm[0, r:16:4, :])
 
         picked_sc = {name: keep.tile([P, S], U8, name="picked_sc_" + name, align_bytes=64) for name in "iec"}
         picked_w = {}
-        reuse = {("c", 0, 1): ("i", 0, 0), ("e", 0, 1): ("i", 0, 1), ("c", 1, 1): ("i", 1, 0), ("e", 1, 1): ("i", 1, 1)}
+        reuse = {("c", 0, 1): ("i", 0, 0), ("c", 1, 1): ("i", 0, 1), ("e", 0, 0): ("i", 1, 0), ("e", 0, 1): ("i", 1, 1)}
 
         def gather_scales(name):
             nc.vector.tensor_copy(picked_sc[name][:], tab_sc[:].bitcast(U8).indirect(lists[name][:]))
@@ -166,14 +166,19 @@ def tile_list_inhibited_enzyme_fluxes_kernel(
             root = ring.tile([P, H], F32)
             nc.scalar.activation(root[:], squares[blk][:], ACT.Abs_reciprocal_sqrt, bias=1.0)
             damp[blk] = ring.tile([P, H], F32, name="damp", bufs=BLOCKS)
-            if blk in ():
+            if blk in (0,2,4,6,):
                 nc.gpsimd.tensor_tensor(damp[blk][:], root[:], root[:], MULT)
             else:
                 nc.scalar.activation(damp[blk][:], root[:], ACT.Square)
 
         def damp_substrate(blk):
             damped[blk] = ring.tile([P, H], F32, name="damped", bufs=BLOCKS)
-            nc.vector.tensor_tensor(as_pairs(damped[blk]), sums["c", blk], as_pairs(damp[blk]), MULT)
+            if blk in ():
+                level = ring.tile([P, H], F32)
+                nc.scalar.copy(as_pairs(level), sums["c", blk])
+                nc.gpsimd.tensor_tensor(damped[blk][:], level[:], damp[blk][:], MULT)
+            else:
+                nc.vector.tensor_tensor(as_pairs(damped[blk]), sums["c", blk], as_pairs(damp[blk]), MULT)
             give_bank(("c", blk))
 
         def rate(blk):
@@ -203,7 +208,7 @@ def tile_list_inhibited_enzyme_fluxes_kernel(
             width = len(group) * BLOCK
             st_bytes = st_w[:].bitcast(U8)
             st_plane = st_sc[:].bitcast(U8)
-            shared = group[-1] >= 1
+            shared = group[-1] >= 6
             per_bank = 2 if shared else H // width
             result = ring.tile([P, N // P, width], F32, bufs=BLOCKS)
             for first in range(0, N // P, per_bank):
@@ -219,8 +224,8 @@ def tile_list_inhibited_enzyme_fluxes_kernel(
                     for c in range(first, first + per_bank):
                         nc.scalar.activation(result[:, c, :], y[:, c - first, :], ACT.Identity, bias=bias[:, c : c + 1])
                 give_bank("y")
-            cols = out[:, group[0] * BLOCK : group[0] * BLOCK + width]
-            nc.sync.dma_start(cols.rearrange("(c p) j -> p c j", p=P), result[:])
+                rows = out[first * P : (first + per_bank) * P, group[0] * BLOCK : group[0] * BLOCK + width]
+                nc.sync.dma_start(rows.rearrange("(c p) j -> p c j", p=P), result[:, first : first + per_bank, :])
 
         gather_scales("i")
         gather_scales("c")
@@ -229,39 +234,39 @@ def tile_list_inhibited_enzyme_fluxes_kernel(
         gather_words("i", 0, 0)
         gather_words("c", 0, 0)
         gather_words("i", 0, 1)
-        gather_words("e", 0, 0)
         gather_words("i", 1, 0)
         gather_words("i", 1, 1)
         nc.scalar.copy(we_bf[:, 0], we_raw[0][:].rearrange("p j r -> p r j"))
         for blk in range(BLOCKS):
             multiply("i", blk)
             square_inhibitor(blk)
-            if blk < 0:
+            if blk < 1:
                 damping(blk)
         gather_words("c", 1, 0)
+        gather_words("e", 0, 0)
         gather_words("e", 1, 0)
-        nc.vector.tensor_copy(we_bf[:, 1], we_raw[1][:].rearrange("p j r -> p r j"))
+        nc.gpsimd.tensor_scalar(we_bf[:, 1], we_raw[1][:].rearrange("p j r -> p r j"), 1.0, 0.0, MULT, ADD)
         quantise_we()
         gather_words("c", 0, 1)
         gather_words("c", 1, 1)
         gather_words("e", 0, 1)
         gather_words("e", 1, 1)
-        groups = {group[-1]: group for group in [(0,),(1,),(2,),(3,),(4,),(5,),(6,),(7,)]}
-        dampings = list(range(0, BLOCKS))
+        groups = {group[-1]: group for group in [(0, 1),(2, 3),(4, 5),(6, 7)]}
+        dampings = list(range(1, BLOCKS))
         for step in range(-6, 2 * BLOCKS):
-            while dampings and dampings[0] <= step + 3:
+            while dampings and dampings[0] <= step + 2:
                 damping(dampings.pop(0))
-            if 0 <= step + 3 < BLOCKS:
-                multiply("c", step + 3)
+            if 0 <= step + 5 < BLOCKS:
+                multiply("c", step + 5)
             if 0 <= step + 0 < BLOCKS:
                 multiply("e", step + 0)
             if 0 <= step < BLOCKS:
                 damp_substrate(step)
             if 0 <= step - 1 < BLOCKS:
                 rate(step - 1)
-            if step - 3 in groups:
-                turn(groups[step - 3])
+            if step - 2 in groups:
+                turn(groups[step - 2])
             if step - 3 in groups:
                 quantise_rates(groups[step - 3])
-            if step - 5 in groups:
-                flux(groups[step - 5])
+            if step - 4 in groups:
+                flux(groups[step - 4])

@@ -193,7 +193,10 @@ def tile_list_inhibited_enzyme_fluxes_kernel(
                 for u in range(2):
                     nc.tensor.transpose(turned[:, g, u, :], words[:, u * P : (u + 1) * P], ident[:])
             grouped[group] = ring.tile([P, len(group), BLOCK, 4], BF16, name="grouped", align_bytes=64)
-            nc.scalar.copy(grouped[group][:].bitcast(F32), turned[:].rearrange("p g u j -> p g j u"))
+            if group[-1] == BLOCKS - 1:
+                nc.vector.tensor_copy(grouped[group][:].bitcast(F32), turned[:].rearrange("p g u j -> p g j u"))
+            else:
+                nc.scalar.copy(grouped[group][:].bitcast(F32), turned[:].rearrange("p g u j -> p g j u"))
             give_bank("turned")
 
         def quantise_rates(group):
@@ -209,7 +212,7 @@ def tile_list_inhibited_enzyme_fluxes_kernel(
             st_bytes = st_w[:].bitcast(U8)
             st_plane = st_sc[:].bitcast(U8)
             shared = group[-1] >= 6
-            per_bank = 2 if shared else H // width
+            per_bank = 1 if group[0] >= PER else 2
             result = ring.tile([P, N // P, width], F32, bufs=BLOCKS)
             for first in range(0, N // P, per_bank):
                 y = take_bank("y", [per_bank, width])
@@ -217,9 +220,8 @@ def tile_list_inhibited_enzyme_fluxes_kernel(
                     nc.tensor.matmul_mx(out=y[:, c - first, :], lhsT=st_bytes[:, 2 * P * c : 2 * P * (c + 1)].bitcast(FP4X4),
                                         lhsT_scale=st_plane[:, P * c : P * (c + 1)],
                                         rhs=h_w[:].bitcast(FP8X4), rhs_scale=h_sc[:], start=True, stop=True)
-                if shared and first > 0:
-                    spread = bias[:, first : first + per_bank].unsqueeze(2).to_broadcast([P, per_bank, width])
-                    nc.vector.tensor_tensor(result[:, first : first + per_bank, :], y[:], spread, ADD)
+                if shared and first % 2 == 1:
+                    nc.vector.tensor_scalar(result[:, first, :], y[:, 0, :], bias[:, first : first + 1], None, ADD)
                 else:
                     for c in range(first, first + per_bank):
                         nc.scalar.activation(result[:, c, :], y[:, c - first, :], ACT.Identity, bias=bias[:, c : c + 1])

@@ -46,9 +46,9 @@ def tile_list_inhibited_enzyme_fluxes_kernel(
         wi_sc = keep.tile([P, PASSES, H // 4], I32, align_bytes=64)
         ws_sc = keep.tile([P, PASSES, H // 4], I32, align_bytes=64)
         st_sc = keep.tile([P, N // 4], I32, align_bytes=64)
-        we_raw = [keep.tile([P, 4, H], F32, name="we_raw%d" % a) for a in range(PASSES)]
+        we_raw = [keep.tile([P, 4, H], F32, name="we_raw%d" % a, tag="we_raw%d" % a) for a in range(PASSES)]
         bias = keep.tile([P, N // P], F32)
-        shifted = keep.tile([P, S // 4], I32, align_bytes=64)
+        shifted = {name: keep.tile([P, S // 4], I32, name="shifted_" + name, align_bytes=64) for name in "iec"}
         ident = keep.tile([P, P], F32)
         warm_in = keep.tile([P, 1], F32)
         warm_out = keep.tile([P, 1], F32)
@@ -59,17 +59,16 @@ def tile_list_inhibited_enzyme_fluxes_kernel(
         nc.vector.memset(wi_sc[:], 0)
         nc.vector.memset(ws_sc[:], 0)
         nc.vector.memset(st_sc[:], 0)
-        nc.vector.memset(shifted[:], 0)
+        for name in "iec":
+            nc.vector.memset(shifted[name][:], 0)
         make_identity(nc, ident[:])
 
         nc.sync.dma_start(lists["i"][:], offs3)
+        nc.sync.dma_start(wi_w[:], wi8_words.rearrange("a p y i -> p a (y i)").bitcast(I32))
         nc.sync.dma_start(lists["c"][:], offs2)
-        nc.sync.dma_start(lists["e"][:], offs)
-        nc.sync.dma_start(st_w[:], st4_words[0].bitcast(I32))
         tab_sc_hbm = tab_scales.bitcast(I32)
         for r in range(4):
-            for a in range(PASSES):
-                nc.sync.dma_start(tab_sc[4 * a + r : P : 32, :], tab_sc_hbm[a, r:16:4, :])
+            nc.sync.dma_start(tab_sc[r:P:16, :], tab_sc_hbm[:, r:16:4, :].rearrange("a q n -> q a n"))
 
         def load_tab(a):
             nc.sync.dma_start(tab_w[a][:], tab_words[a].rearrange("p t i -> p (t i)").bitcast(I32))
@@ -83,13 +82,14 @@ def tile_list_inhibited_enzyme_fluxes_kernel(
             nc.sync.dma_start(we_raw[a][:], we[512 * a : 512 * (a + 1), :].rearrange("(p j) r -> p j r", j=4))
 
         load_tab(0)
-        load_tab(1)
-        load_we(0)
-        nc.sync.dma_start(wi_w[:], wi8_words.rearrange("a p y i -> p a (y i)").bitcast(I32))
         load_planes(wi_sc, wi8_scales)
-        load_we(1)
+        load_tab(1)
+        nc.sync.dma_start(lists["e"][:], offs)
         nc.sync.dma_start(ws_w[:], ws4_words.rearrange("a p y -> p a y").bitcast(I32))
         load_planes(ws_sc, ws4_scales)
+        load_we(0)
+        load_we(1)
+        nc.sync.dma_start(st_w[:], st4_words[0].bitcast(I32))
         with nc.allow_non_contiguous_dma(reason="one bias value a partition"):
             nc.sync.dma_start(bias[:], b.rearrange("(c p) -> p c", p=P))
         st_sc_hbm = st4_scales.bitcast(I32)
@@ -98,25 +98,27 @@ def tile_list_inhibited_enzyme_fluxes_kernel(
 
         picked_sc = {name: keep.tile([P, S], U8, name="picked_sc_" + name, align_bytes=64) for name in "iec"}
         picked_w = {}
-        reuse = {("c", 0, 1): ("i", 0, 0), ("c", 1, 1): ("i", 0, 1), ("e", 0, 0): ("i", 1, 0), ("e", 0, 1): ("i", 1, 1)}
 
         def gather_scales(name):
             nc.vector.tensor_copy(picked_sc[name][:], tab_sc[:].bitcast(U8).indirect(lists[name][:]))
+            (nc.sync if name == "e" else nc.gpsimd).dma_start(shifted[name][0 : P - 16, :], picked_sc[name][16:P, :].bitcast(I32))
 
         def gather_words(name, a, ch):
             cols = slice(ch * CHUNK // 16, (ch + 1) * CHUNK // 16)
-            slot = "picked_w_%s%d%d" % reuse.get((name, a, ch), (name, a, ch))
-            picked_w[name, a, ch] = keep.tile([P, CHUNK], U32, name=slot, tag=slot, align_bytes=64)
+            slot = "we_bf%d" % a if (name, ch) == ("e", 0) else "picked_w_%s%d%d" % (name, a, ch)
+            picked_w[name, a, ch] = keep.tile([P, CHUNK], U32, name="picked_w_%s%d%d" % (name, a, ch), tag=slot, align_bytes=64)
             nc.vector.tensor_copy(picked_w[name, a, ch][:], tab_w[a][:].bitcast(U32).indirect(lists[name][:, cols]))
 
-        we_bf = keep.tile([P, PASSES, H, 4], BF16, align_bytes=64)
+        we_bf = [keep.tile([P, H, 4], BF16, name="we_bf%d" % a, tag="we_bf%d" % a, align_bytes=64) for a in range(PASSES)]
         we_w = keep.tile([P, PASSES, H], U32, align_bytes=64)
         we_sc = keep.tile([P, PASSES, H], U8, align_bytes=64)
 
-        def quantise_we():
-            nc.vector.quantize_mx(out=we_w[:].rearrange("p a r -> p (a r)").bitcast(FP8X4),
-                                  scales=we_sc[:].rearrange("p a r -> p (a r)"),
-                                  in_=we_bf[:].rearrange("p a r j -> p (a r j)"))
+        def round_we(a):
+            nc.gpsimd.tensor_scalar(we_bf[a][:], we_raw[a][:].rearrange("p j r -> p r j"), 1.0, 0.0, MULT, ADD)
+
+        def quantise_we(a):
+            nc.vector.quantize_mx(out=we_w[:, a, :].bitcast(FP8X4), scales=we_sc[:, a, :],
+                                  in_=we_bf[a][:].rearrange("p r j -> p (r j)"))
 
         free_banks = list(range(8))
         held = {}
@@ -135,12 +137,11 @@ def tile_list_inhibited_enzyme_fluxes_kernel(
             all_cols = slice(blk * BLOCK, (blk + 1) * BLOCK)
             acc = take_bank((name, blk), [H])
             for a in range(PASSES):
+                plane = picked_sc[name][:, all_cols] if a == 0 else shifted[name][:].bitcast(U8)[:, all_cols]
                 if name == "c":
-                    plane = picked_sc["c"][:, all_cols] if a == 0 else shifted[:].bitcast(U8)[:, all_cols]
                     rhs = ws_w[:, a, :].bitcast(U8).bitcast(FP4X4)
                     rhs_scale = ws_sc[:, a, :].bitcast(U8)
                 else:
-                    plane = picked_sc[name][4 * a :, all_cols]
                     rhs = (wi_w if name == "i" else we_w)[:, a, :].bitcast(FP8X4)
                     rhs_scale = wi_sc[:, a, :].bitcast(U8) if name == "i" else we_sc[:, a, :]
                 nc.tensor.matmul_mx(out=acc[:], lhsT=picked_w[name, a, ch][:, cols].bitcast(FP8X4), lhsT_scale=plane,
@@ -162,23 +163,24 @@ def tile_list_inhibited_enzyme_fluxes_kernel(
             nc.scalar.activation(as_pairs(squares[blk]), sums["i", blk], ACT.Square)
             give_bank(("i", blk))
 
-        def damping(blk):
+        def damping(blk, on_gpsimd):
             root = ring.tile([P, H], F32)
             nc.scalar.activation(root[:], squares[blk][:], ACT.Abs_reciprocal_sqrt, bias=1.0)
-            damp[blk] = ring.tile([P, H], F32, name="damp", bufs=BLOCKS)
-            if blk in (0,2,4,6,):
-                nc.gpsimd.tensor_tensor(damp[blk][:], root[:], root[:], MULT)
+            if on_gpsimd:
+                damp[blk] = late_damp[:, blk, :]
+                nc.gpsimd.tensor_tensor(damp[blk], root[:], root[:], MULT)
             else:
-                nc.scalar.activation(damp[blk][:], root[:], ACT.Square)
+                damp[blk] = ring.tile([P, H], F32, name="damp", bufs=PER)[:]
+                nc.scalar.activation(damp[blk], root[:], ACT.Square)
 
-        def damp_substrate(blk):
+        def damp_substrate(blk, on_gpsimd):
             damped[blk] = ring.tile([P, H], F32, name="damped", bufs=BLOCKS)
-            if blk in ():
+            if on_gpsimd:
                 level = ring.tile([P, H], F32)
                 nc.scalar.copy(as_pairs(level), sums["c", blk])
-                nc.gpsimd.tensor_tensor(damped[blk][:], level[:], damp[blk][:], MULT)
+                nc.gpsimd.tensor_tensor(damped[blk][:], level[:], damp[blk], MULT)
             else:
-                nc.vector.tensor_tensor(as_pairs(damped[blk]), sums["c", blk], as_pairs(damp[blk]), MULT)
+                nc.vector.tensor_tensor(as_pairs(damped[blk]), sums["c", blk], damp[blk].rearrange("p (u m e) -> p u m e", u=2, e=2), MULT)
             give_bank(("c", blk))
 
         def rate(blk):
@@ -186,14 +188,14 @@ def tile_list_inhibited_enzyme_fluxes_kernel(
             nc.vector.tensor_tensor(as_pairs(rates[blk]), sums["e", blk], as_pairs(damped[blk]), MULT)
             give_bank(("e", blk))
 
-        def turn(group):
+        def turn(group, on_vector=False):
             turned = take_bank("turned", [len(group), 2, BLOCK])
             for g, blk in enumerate(group):
                 words = rates[blk][:].bitcast(F32)
                 for u in range(2):
                     nc.tensor.transpose(turned[:, g, u, :], words[:, u * P : (u + 1) * P], ident[:])
             grouped[group] = ring.tile([P, len(group), BLOCK, 4], BF16, name="grouped", align_bytes=64)
-            if group[-1] == BLOCKS - 1:
+            if on_vector:
                 nc.vector.tensor_copy(grouped[group][:].bitcast(F32), turned[:].rearrange("p g u j -> p g j u"))
             else:
                 nc.scalar.copy(grouped[group][:].bitcast(F32), turned[:].rearrange("p g u j -> p g j u"))
@@ -206,69 +208,84 @@ def tile_list_inhibited_enzyme_fluxes_kernel(
                                   in_=grouped[group][:].rearrange("p g j t -> p (g j t)"))
             h_mx[group] = h_w, h_sc
 
-        def flux(group):
+        def flux(group, shared=False):
             h_w, h_sc = h_mx[group]
             width = len(group) * BLOCK
             st_bytes = st_w[:].bitcast(U8)
             st_plane = st_sc[:].bitcast(U8)
-            shared = group[-1] >= 6
-            per_bank = 1 if group[0] >= PER else 2
             result = ring.tile([P, N // P, width], F32, bufs=BLOCKS)
-            for first in range(0, N // P, per_bank):
-                y = take_bank("y", [per_bank, width])
-                for c in range(first, first + per_bank):
+            for first in range(0, N // P, 2):
+                y = take_bank("y", [2, width])
+                for c in range(first, first + 2):
                     nc.tensor.matmul_mx(out=y[:, c - first, :], lhsT=st_bytes[:, 2 * P * c : 2 * P * (c + 1)].bitcast(FP4X4),
                                         lhsT_scale=st_plane[:, P * c : P * (c + 1)],
                                         rhs=h_w[:].bitcast(FP8X4), rhs_scale=h_sc[:], start=True, stop=True)
-                if shared and first % 2 == 1:
-                    nc.vector.tensor_scalar(result[:, first, :], y[:, 0, :], bias[:, first : first + 1], None, ADD)
-                else:
-                    for c in range(first, first + per_bank):
+                for c in range(first, first + 2):
+                    if shared and first > 0:
+                        nc.vector.tensor_scalar(result[:, c, :], y[:, c - first, :], bias[:, c : c + 1], None, ADD)
+                    else:
                         nc.scalar.activation(result[:, c, :], y[:, c - first, :], ACT.Identity, bias=bias[:, c : c + 1])
                 give_bank("y")
-                rows = out[first * P : (first + per_bank) * P, group[0] * BLOCK : group[0] * BLOCK + width]
-                nc.sync.dma_start(rows.rearrange("(c p) j -> p c j", p=P), result[:, first : first + per_bank, :])
+                rows = out[first * P : (first + 2) * P, group[0] * BLOCK : group[0] * BLOCK + width]
+                nc.sync.dma_start(rows.rearrange("(c p) j -> p c j", p=P), result[:, first : first + 2, :])
 
         gather_scales("i")
         gather_scales("c")
-        nc.gpsimd.dma_start(shifted[0 : P - 4, :], picked_sc["c"][4:P, :].bitcast(I32))
+        for a in range(PASSES):
+            for name in "ic":
+                for ch in range(CHUNKS):
+                    gather_words(name, a, ch)
         gather_scales("e")
-        gather_words("i", 0, 0)
-        gather_words("c", 0, 0)
-        gather_words("i", 0, 1)
-        gather_words("i", 1, 0)
-        gather_words("i", 1, 1)
-        nc.scalar.copy(we_bf[:, 0], we_raw[0][:].rearrange("p j r -> p r j"))
-        for blk in range(BLOCKS):
-            multiply("i", blk)
-            square_inhibitor(blk)
-            if blk < 1:
-                damping(blk)
-        gather_words("c", 1, 0)
-        gather_words("e", 0, 0)
-        gather_words("e", 1, 0)
-        nc.gpsimd.tensor_scalar(we_bf[:, 1], we_raw[1][:].rearrange("p j r -> p r j"), 1.0, 0.0, MULT, ADD)
-        quantise_we()
-        gather_words("c", 0, 1)
-        gather_words("c", 1, 1)
         gather_words("e", 0, 1)
         gather_words("e", 1, 1)
-        groups = {group[-1]: group for group in [(0, 1),(2, 3),(4, 5),(6, 7)]}
-        dampings = list(range(1, BLOCKS))
-        for step in range(-6, 2 * BLOCKS):
-            while dampings and dampings[0] <= step + 2:
-                damping(dampings.pop(0))
-            if 0 <= step + 5 < BLOCKS:
-                multiply("c", step + 5)
-            if 0 <= step + 0 < BLOCKS:
-                multiply("e", step + 0)
-            if 0 <= step < BLOCKS:
-                damp_substrate(step)
-            if 0 <= step - 1 < BLOCKS:
-                rate(step - 1)
-            if step - 2 in groups:
-                turn(groups[step - 2])
-            if step - 3 in groups:
-                quantise_rates(groups[step - 3])
-            if step - 4 in groups:
-                flux(groups[step - 4])
+        for blk in range(BLOCKS):
+            multiply("i", blk)
+        for blk in range(BLOCKS):
+            square_inhibitor(blk)
+        round_we(0)
+        round_we(1)
+        late_damp = keep.tile([P, PER, H], F32, tag="we_raw1")
+        quantise_we(0)
+        quantise_we(1)
+        gather_words("e", 0, 0)
+        gather_words("e", 1, 0)
+        for blk in range(BLOCKS):
+            multiply("c", blk)
+        for blk in range(PER):
+            damping(blk, True)
+            damp_substrate(blk, True)
+        for blk in range(PER, BLOCKS):
+            multiply("e", blk)
+        for blk in range(PER, BLOCKS):
+            damping(blk, False)
+        damp_substrate(4, False)
+        multiply("e", 0)
+        rate(4)
+        damp_substrate(5, False)
+        multiply("e", 1)
+        rate(5)
+        turn((4, 5))
+        damp_substrate(6, False)
+        multiply("e", 2)
+        rate(6)
+        quantise_rates((4, 5))
+        flux((4, 5))
+        damp_substrate(7, False)
+        multiply("e", 3)
+        rate(7)
+        turn((6, 7))
+        rate(0)
+        rate(1)
+        turn((0, 1))
+        quantise_rates((6, 7))
+        flux((6, 7))
+        rate(2)
+        turn((2,))
+        rate(3)
+        turn((3,), True)
+        quantise_rates((0, 1))
+        flux((0, 1))
+        quantise_rates((2,))
+        flux((2,), True)
+        quantise_rates((3,))
+        flux((3,), True)

@@ -35,6 +35,7 @@ def tile_list_inhibited_enzyme_fluxes_kernel(
     with ExitStack() as ctx:
         keep = ctx.enter_context(tc.tile_pool(name="keep", bufs=1))
         ring = ctx.enter_context(tc.tile_pool(name="ring", bufs=6))
+        reused = ctx.enter_context(tc.tile_pool(name="reused", bufs=1))
         psum = ctx.enter_context(tc.psum_pool(name="psum", bufs=1))
 
         lists = {name: keep.tile([P, S // 16], U16, name="list_" + name) for name in "iec"}
@@ -61,7 +62,11 @@ def tile_list_inhibited_enzyme_fluxes_kernel(
         nc.vector.memset(st_sc[:], 0)
         for name in "iec":
             nc.vector.memset(shifted[name][:], 0)
-        make_identity(nc, ident[:])
+        nc.vector.memset(ident[:], 0.0)
+        make_identity(nc, ident[:], nomemset=True)
+
+        def load_tab(a):
+            nc.sync.dma_start(tab_w[a][:], tab_words[a].rearrange("p t i -> p (t i)").bitcast(I32))
 
         nc.sync.dma_start(lists["i"][:], offs3)
         nc.sync.dma_start(wi_w[:], wi8_words.rearrange("a p y i -> p a (y i)").bitcast(I32))
@@ -69,9 +74,6 @@ def tile_list_inhibited_enzyme_fluxes_kernel(
         tab_sc_hbm = tab_scales.bitcast(I32)
         for r in range(4):
             nc.sync.dma_start(tab_sc[r:P:16, :], tab_sc_hbm[:, r:16:4, :].rearrange("a q n -> q a n"))
-
-        def load_tab(a):
-            nc.sync.dma_start(tab_w[a][:], tab_words[a].rearrange("p t i -> p (t i)").bitcast(I32))
 
         def load_planes(tile, scales):
             hbm = scales.bitcast(I32)
@@ -85,9 +87,9 @@ def tile_list_inhibited_enzyme_fluxes_kernel(
         load_planes(wi_sc, wi8_scales)
         load_tab(1)
         nc.sync.dma_start(lists["e"][:], offs)
+        load_we(0)
         nc.sync.dma_start(ws_w[:], ws4_words.rearrange("a p y -> p a y").bitcast(I32))
         load_planes(ws_sc, ws4_scales)
-        load_we(0)
         load_we(1)
         nc.sync.dma_start(st_w[:], st4_words[0].bitcast(I32))
         with nc.allow_non_contiguous_dma(reason="one bias value a partition"):
@@ -103,22 +105,23 @@ def tile_list_inhibited_enzyme_fluxes_kernel(
             nc.vector.tensor_copy(picked_sc[name][:], tab_sc[:].bitcast(U8).indirect(lists[name][:]))
             (nc.sync if name == "e" else nc.gpsimd).dma_start(shifted[name][0 : P - 16, :], picked_sc[name][16:P, :].bitcast(I32))
 
-        def gather_words(name, a, ch):
+        def gather_words(name, a, ch, into=None):
             cols = slice(ch * CHUNK // 16, (ch + 1) * CHUNK // 16)
-            slot = "we_bf%d" % a if (name, ch) == ("e", 0) else "picked_w_%s%d%d" % (name, a, ch)
-            picked_w[name, a, ch] = keep.tile([P, CHUNK], U32, name="picked_w_%s%d%d" % (name, a, ch), tag=slot, align_bytes=64)
-            nc.vector.tensor_copy(picked_w[name, a, ch][:], tab_w[a][:].bitcast(U32).indirect(lists[name][:, cols]))
+            if into is None:
+                into = keep.tile([P, CHUNK], U32, name="picked_w_%s%d%d" % (name, a, ch), align_bytes=64)[:]
+            picked_w[name, a, ch] = into
+            nc.vector.tensor_copy(into, tab_w[a][:].bitcast(U32).indirect(lists[name][:, cols]))
 
-        we_bf = [keep.tile([P, H, 4], BF16, name="we_bf%d" % a, tag="we_bf%d" % a, align_bytes=64) for a in range(PASSES)]
         we_w = keep.tile([P, PASSES, H], U32, align_bytes=64)
         we_sc = keep.tile([P, PASSES, H], U8, align_bytes=64)
 
         def round_we(a):
-            nc.gpsimd.tensor_scalar(we_bf[a][:], we_raw[a][:].rearrange("p j r -> p r j"), 1.0, 0.0, MULT, ADD)
+            nc.gpsimd.tensor_scalar(we_bf[:, a], we_raw[a][:].rearrange("p j r -> p r j"), 1.0, 0.0, MULT, ADD)
 
-        def quantise_we(a):
-            nc.vector.quantize_mx(out=we_w[:, a, :].bitcast(FP8X4), scales=we_sc[:, a, :],
-                                  in_=we_bf[a][:].rearrange("p r j -> p (r j)"))
+        def quantise_we():
+            nc.vector.quantize_mx(out=we_w[:].rearrange("p a r -> p (a r)").bitcast(FP8X4),
+                                  scales=we_sc[:].rearrange("p a r -> p (a r)"),
+                                  in_=we_bf[:].rearrange("p a r j -> p (a r j)"))
 
         free_banks = list(range(8))
         held = {}
@@ -131,12 +134,15 @@ def tile_list_inhibited_enzyme_fluxes_kernel(
             free_banks.append(held.pop(key))
 
         sums = {}
+        banks = {}
 
-        def multiply(name, blk):
+        def multiply(name, blk, passes=range(PASSES)):
             ch, cols = blk // PER, slice((blk % PER) * BLOCK, (blk % PER + 1) * BLOCK)
             all_cols = slice(blk * BLOCK, (blk + 1) * BLOCK)
-            acc = take_bank((name, blk), [H])
-            for a in range(PASSES):
+            if 0 in passes:
+                banks[name, blk] = take_bank((name, blk), [H])
+            acc = banks[name, blk]
+            for a in passes:
                 plane = picked_sc[name][:, all_cols] if a == 0 else shifted[name][:].bitcast(U8)[:, all_cols]
                 if name == "c":
                     rhs = ws_w[:, a, :].bitcast(U8).bitcast(FP4X4)
@@ -149,7 +155,7 @@ def tile_list_inhibited_enzyme_fluxes_kernel(
             sums[name, blk] = acc[:].rearrange("p (m u e) -> p u m e", u=2, e=2)
 
         def as_pairs(tile):
-            return tile[:].rearrange("p (u m e) -> p u m e", u=2, e=2)
+            return tile[:, :].rearrange("p (u m e) -> p u m e", u=2, e=2)
 
         squares = {}
         damp = {}
@@ -163,24 +169,23 @@ def tile_list_inhibited_enzyme_fluxes_kernel(
             nc.scalar.activation(as_pairs(squares[blk]), sums["i", blk], ACT.Square)
             give_bank(("i", blk))
 
-        def damping(blk, on_gpsimd):
-            root = ring.tile([P, H], F32)
+        def damping(blk, on_gpsimd, into=None):
+            root = ring.tile([P, H], F32, name="root")
             nc.scalar.activation(root[:], squares[blk][:], ACT.Abs_reciprocal_sqrt, bias=1.0)
+            damp[blk] = ring.tile([P, H], F32, name="damp", bufs=BLOCKS)[:] if into is None else into
             if on_gpsimd:
-                damp[blk] = late_damp[:, blk, :]
                 nc.gpsimd.tensor_tensor(damp[blk], root[:], root[:], MULT)
             else:
-                damp[blk] = ring.tile([P, H], F32, name="damp", bufs=PER)[:]
                 nc.scalar.activation(damp[blk], root[:], ACT.Square)
 
-        def damp_substrate(blk, on_gpsimd):
-            damped[blk] = ring.tile([P, H], F32, name="damped", bufs=BLOCKS)
+        def damp_substrate(blk, on_gpsimd, into=None):
+            damped[blk] = ring.tile([P, H], F32, name="damped", bufs=BLOCKS)[:] if into is None else into
             if on_gpsimd:
                 level = ring.tile([P, H], F32)
                 nc.scalar.copy(as_pairs(level), sums["c", blk])
-                nc.gpsimd.tensor_tensor(damped[blk][:], level[:], damp[blk], MULT)
+                nc.gpsimd.tensor_tensor(damped[blk], level[:], damp[blk], MULT)
             else:
-                nc.vector.tensor_tensor(as_pairs(damped[blk]), sums["c", blk], damp[blk].rearrange("p (u m e) -> p u m e", u=2, e=2), MULT)
+                nc.vector.tensor_tensor(as_pairs(damped[blk]), sums["c", blk], as_pairs(damp[blk]), MULT)
             give_bank(("c", blk))
 
         def rate(blk):
@@ -235,50 +240,58 @@ def tile_list_inhibited_enzyme_fluxes_kernel(
             for name in "ic":
                 for ch in range(CHUNKS):
                     gather_words(name, a, ch)
+            for blk in range(BLOCKS):
+                multiply("i", blk, [a])
         gather_scales("e")
         gather_words("e", 0, 1)
-        gather_words("e", 1, 1)
-        for blk in range(BLOCKS):
-            multiply("i", blk)
         for blk in range(BLOCKS):
             square_inhibitor(blk)
+        we_bf = reused.tile([P, PASSES, H, 4], BF16, offset=0, align_bytes=64)
         round_we(0)
         round_we(1)
-        late_damp = keep.tile([P, PER, H], F32, tag="we_raw1")
-        quantise_we(0)
-        quantise_we(1)
-        gather_words("e", 0, 0)
-        gather_words("e", 1, 0)
-        for blk in range(BLOCKS):
+        quantise_we()
+        late_words = reused.tile([P, 3, CHUNK], U32, offset=0, align_bytes=64)
+        late_floats = reused.tile([P, 3, H], F32, offset=6144, align_bytes=64)
+        gather_words("e", 1, 1, late_words[:, 0, :])
+        gather_words("e", 0, 0, late_words[:, 1, :])
+        gather_words("e", 1, 0, late_words[:, 2, :])
+        for blk in (0, 1, 4, 5, 6, 7, 2, 3):
             multiply("c", blk)
-        for blk in range(PER):
-            damping(blk, True)
+        for blk in (0, 1):
+            damping(blk, True, late_floats[:, blk, :])
             damp_substrate(blk, True)
-        for blk in range(PER, BLOCKS):
+        for blk in (4, 5):
             multiply("e", blk)
-        for blk in range(PER, BLOCKS):
+        for blk in (4, 5):
+            damping(blk, False)
+        damping(2, True, late_floats[:, 2, :])
+        for blk in (6, 7, 3):
             damping(blk, False)
         damp_substrate(4, False)
-        multiply("e", 0)
-        rate(4)
+        multiply("e", 6)
         damp_substrate(5, False)
-        multiply("e", 1)
+        multiply("e", 7)
+        rate(4)
+        multiply("e", 0)
         rate(5)
         turn((4, 5))
         damp_substrate(6, False)
-        multiply("e", 2)
+        multiply("e", 1)
         rate(6)
+        damp_substrate(7, False)
         quantise_rates((4, 5))
         flux((4, 5))
-        damp_substrate(7, False)
-        multiply("e", 3)
         rate(7)
         turn((6, 7))
+        multiply("e", 2)
         rate(0)
+        multiply("e", 3)
         rate(1)
         turn((0, 1))
         quantise_rates((6, 7))
         flux((6, 7))
+        damp_substrate(2, False)
+        damp_substrate(3, False)
         rate(2)
         turn((2,))
         rate(3)

@@ -123,24 +123,17 @@ def tile_list_inhibited_enzyme_fluxes_kernel(
                                   scales=we_sc[:].rearrange("p a r -> p (a r)"),
                                   in_=we_bf[:].rearrange("p a r j -> p (a r j)"))
 
-        free_banks = list(range(8))
-        held = {}
-
-        def take_bank(key, shape):
-            held[key] = free_banks.pop(0)
-            return psum.tile([P] + shape, F32, name="bank%d" % held[key], tag="bank%d" % held[key])
-
-        def give_bank(key):
-            free_banks.append(held.pop(key))
+        def take_bank(bank, shape):
+            return psum.tile([P] + shape, F32, name="bank%d" % bank, tag="bank%d" % bank)
 
         sums = {}
         banks = {}
 
-        def multiply(name, blk, passes=range(PASSES)):
+        def multiply(name, blk, bank, passes=range(PASSES)):
             ch, cols = blk // PER, slice((blk % PER) * BLOCK, (blk % PER + 1) * BLOCK)
             all_cols = slice(blk * BLOCK, (blk + 1) * BLOCK)
             if 0 in passes:
-                banks[name, blk] = take_bank((name, blk), [H])
+                banks[name, blk] = take_bank(bank, [H])
             acc = banks[name, blk]
             for a in passes:
                 plane = picked_sc[name][:, all_cols] if a == 0 else shifted[name][:].bitcast(U8)[:, all_cols]
@@ -157,54 +150,63 @@ def tile_list_inhibited_enzyme_fluxes_kernel(
         def as_pairs(tile):
             return tile[:, :].rearrange("p (u m e) -> p u m e", u=2, e=2)
 
-        squares = {}
         damp = {}
+        levels = {}
         damped = {}
         rates = {}
         grouped = {}
+        place = {}
         h_mx = {}
 
+        squares = [keep.tile([P, 2, H], F32, name="squares%d" % pair) for pair in range(BLOCKS // 2)]
+        roots = [keep.tile([P, 2, H], F32, name="roots%d" % pair) for pair in range(BLOCKS // 2)]
+
         def square_inhibitor(blk):
-            squares[blk] = ring.tile([P, H], F32, name="square", bufs=BLOCKS)
-            nc.scalar.activation(as_pairs(squares[blk]), sums["i", blk], ACT.Square)
-            give_bank(("i", blk))
+            nc.scalar.activation(as_pairs(squares[blk // 2][:, blk % 2, :]), sums["i", blk], ACT.Square)
 
-        def damping(blk, on_gpsimd, into=None):
-            root = ring.tile([P, H], F32, name="root")
-            nc.scalar.activation(root[:], squares[blk][:], ACT.Abs_reciprocal_sqrt, bias=1.0)
-            damp[blk] = ring.tile([P, H], F32, name="damp", bufs=BLOCKS)[:] if into is None else into
-            if on_gpsimd:
-                nc.gpsimd.tensor_tensor(damp[blk], root[:], root[:], MULT)
+        def inverse_root(first):
+            nc.scalar.activation(roots[first // 2][:], squares[first // 2][:], ACT.Abs_reciprocal_sqrt, bias=1.0)
+
+        def damping(first, count, into=None):
+            root = roots[first // 2][:, first % 2 : first % 2 + count, :]
+            if into is None:
+                into = keep.tile([P, count, H], F32, name="damp%d" % first)[:]
+                nc.scalar.activation(into, root, ACT.Square)
             else:
-                nc.scalar.activation(damp[blk], root[:], ACT.Square)
+                nc.gpsimd.tensor_tensor(into, root, root, MULT)
+            for g in range(count):
+                damp[first + g] = into[:, g, :]
 
-        def damp_substrate(blk, on_gpsimd, into=None):
-            damped[blk] = ring.tile([P, H], F32, name="damped", bufs=BLOCKS)[:] if into is None else into
+        def copy_substrate(blk):
+            levels[blk] = ring.tile([P, H], F32, name="level")
+            nc.scalar.copy(as_pairs(levels[blk]), sums["c", blk])
+
+        def damp_substrate(blk, on_gpsimd):
+            damped[blk] = ring.tile([P, H], F32, name="damped", bufs=BLOCKS)[:]
             if on_gpsimd:
-                level = ring.tile([P, H], F32)
-                nc.scalar.copy(as_pairs(level), sums["c", blk])
-                nc.gpsimd.tensor_tensor(damped[blk], level[:], damp[blk], MULT)
+                nc.gpsimd.tensor_tensor(damped[blk], levels[blk][:], damp[blk], MULT)
             else:
                 nc.vector.tensor_tensor(as_pairs(damped[blk]), sums["c", blk], as_pairs(damp[blk]), MULT)
-            give_bank(("c", blk))
 
-        def rate(blk):
-            rates[blk] = ring.tile([P, H], BF16, name="rate", align_bytes=64)
+        def rate(blk, behind=None):
+            if behind is None:
+                rates[blk] = ring.tile([P, H], BF16, name="rate", align_bytes=64)
+            else:
+                rates[blk] = reused.tile([P, H], BF16, name="rate%d" % blk, offset=place[behind], align_bytes=64)
             nc.vector.tensor_tensor(as_pairs(rates[blk]), sums["e", blk], as_pairs(damped[blk]), MULT)
-            give_bank(("e", blk))
 
-        def turn(group, on_vector=False):
-            turned = take_bank("turned", [len(group), 2, BLOCK])
+        def turn(group, bank, on_vector=False):
+            turned = take_bank(bank, [len(group), 2, BLOCK])
             for g, blk in enumerate(group):
                 words = rates[blk][:].bitcast(F32)
                 for u in range(2):
                     nc.tensor.transpose(turned[:, g, u, :], words[:, u * P : (u + 1) * P], ident[:])
-            grouped[group] = ring.tile([P, len(group), BLOCK, 4], BF16, name="grouped", align_bytes=64)
+            place[group] = 12288 + 2048 * len(place)
+            grouped[group] = reused.tile([P, len(group), BLOCK, 4], BF16, name="grouped%d" % group[0], offset=place[group], align_bytes=64)
             if on_vector:
                 nc.vector.tensor_copy(grouped[group][:].bitcast(F32), turned[:].rearrange("p g u j -> p g j u"))
             else:
                 nc.scalar.copy(grouped[group][:].bitcast(F32), turned[:].rearrange("p g u j -> p g j u"))
-            give_bank("turned")
 
         def quantise_rates(group):
             h_w = ring.tile([P, len(group) * BLOCK], U32, align_bytes=64)
@@ -213,26 +215,24 @@ def tile_list_inhibited_enzyme_fluxes_kernel(
                                   in_=grouped[group][:].rearrange("p g j t -> p (g j t)"))
             h_mx[group] = h_w, h_sc
 
-        def flux(group, shared=False):
+        def flux(group, first, bank, on_vector=False):
             h_w, h_sc = h_mx[group]
             width = len(group) * BLOCK
             st_bytes = st_w[:].bitcast(U8)
             st_plane = st_sc[:].bitcast(U8)
-            result = ring.tile([P, N // P, width], F32, bufs=BLOCKS)
-            for first in range(0, N // P, 2):
-                y = take_bank("y", [2, width])
+            result = ring.tile([P, 2, width], F32, bufs=10)
+            y = take_bank(bank, [2, width])
+            for c in range(first, first + 2):
+                nc.tensor.matmul_mx(out=y[:, c - first, :], lhsT=st_bytes[:, 2 * P * c : 2 * P * (c + 1)].bitcast(FP4X4),
+                                    lhsT_scale=st_plane[:, P * c : P * (c + 1)],
+                                    rhs=h_w[:].bitcast(FP8X4), rhs_scale=h_sc[:], start=True, stop=True)
+            if on_vector:
+                nc.vector.tensor_tensor(result[:], y[:], bias[:, first : first + 2].unsqueeze(2).to_broadcast([P, 2, width]), ADD)
+            else:
                 for c in range(first, first + 2):
-                    nc.tensor.matmul_mx(out=y[:, c - first, :], lhsT=st_bytes[:, 2 * P * c : 2 * P * (c + 1)].bitcast(FP4X4),
-                                        lhsT_scale=st_plane[:, P * c : P * (c + 1)],
-                                        rhs=h_w[:].bitcast(FP8X4), rhs_scale=h_sc[:], start=True, stop=True)
-                for c in range(first, first + 2):
-                    if shared and first > 0:
-                        nc.vector.tensor_scalar(result[:, c, :], y[:, c - first, :], bias[:, c : c + 1], None, ADD)
-                    else:
-                        nc.scalar.activation(result[:, c, :], y[:, c - first, :], ACT.Identity, bias=bias[:, c : c + 1])
-                give_bank("y")
-                rows = out[first * P : (first + 2) * P, group[0] * BLOCK : group[0] * BLOCK + width]
-                nc.sync.dma_start(rows.rearrange("(c p) j -> p c j", p=P), result[:, first : first + 2, :])
+                    nc.scalar.activation(result[:, c - first, :], y[:, c - first, :], ACT.Identity, bias=bias[:, c : c + 1])
+            rows = out[first * P : (first + 2) * P, group[0] * BLOCK : group[0] * BLOCK + width]
+            nc.sync.dma_start(rows.rearrange("(c p) j -> p c j", p=P), result[:])
 
         gather_scales("i")
         gather_scales("c")
@@ -241,7 +241,7 @@ def tile_list_inhibited_enzyme_fluxes_kernel(
                 for ch in range(CHUNKS):
                     gather_words(name, a, ch)
             for blk in range(BLOCKS):
-                multiply("i", blk, [a])
+                multiply("i", blk, blk, [a])
         gather_scales("e")
         gather_words("e", 0, 1)
         for blk in range(BLOCKS):
@@ -251,54 +251,65 @@ def tile_list_inhibited_enzyme_fluxes_kernel(
         round_we(1)
         quantise_we()
         late_words = reused.tile([P, 3, CHUNK], U32, offset=0, align_bytes=64)
-        late_floats = reused.tile([P, 3, H], F32, offset=6144, align_bytes=64)
+        late_pair = reused.tile([P, 2, H], F32, offset=6144, align_bytes=64)
         gather_words("e", 1, 1, late_words[:, 0, :])
         gather_words("e", 0, 0, late_words[:, 1, :])
         gather_words("e", 1, 0, late_words[:, 2, :])
-        for blk in (0, 1, 4, 5, 6, 7, 2, 3):
-            multiply("c", blk)
-        for blk in (0, 1):
-            damping(blk, True, late_floats[:, blk, :])
-            damp_substrate(blk, True)
-        for blk in (4, 5):
-            multiply("e", blk)
-        for blk in (4, 5):
-            damping(blk, False)
-        damping(2, True, late_floats[:, 2, :])
-        for blk in (6, 7, 3):
-            damping(blk, False)
+        for bank, blk in enumerate((0, 1, 4, 2, 5, 6, 7, 3)):
+            multiply("c", blk, bank)
+        inverse_root(0)
+        damping(0, 2, late_pair[:])
+        copy_substrate(0)
+        damp_substrate(0, True)
+        multiply("e", 4, 0)
+        copy_substrate(1)
+        damp_substrate(1, True)
+        multiply("e", 5, 1)
+        inverse_root(4)
+        copy_substrate(2)
+        multiply("e", 6, 3)
+        inverse_root(2)
+        damping(2, 1, reused.tile([P, 1, H], F32, name="late_single", offset=6144, align_bytes=64)[:])
+        damp_substrate(2, True)
+        damping(4, 2)
+        inverse_root(6)
+        damping(6, 2)
         damp_substrate(4, False)
-        multiply("e", 6)
+        multiply("e", 7, 2)
         damp_substrate(5, False)
-        multiply("e", 7)
+        multiply("e", 0, 4)
         rate(4)
-        multiply("e", 0)
         rate(5)
-        turn((4, 5))
+        turn((4, 5), 0)
+        multiply("e", 1, 1)
+        damping(3, 1)
         damp_substrate(6, False)
-        multiply("e", 1)
         rate(6)
+        multiply("e", 2, 3)
         damp_substrate(7, False)
         quantise_rates((4, 5))
-        flux((4, 5))
-        rate(7)
-        turn((6, 7))
-        multiply("e", 2)
+        flux((4, 5), 0, 5)
+        multiply("e", 3, 0)
+        rate(7, (4, 5))
+        turn((6, 7), 2)
+        flux((4, 5), 2, 6)
         rate(0)
-        multiply("e", 3)
         rate(1)
-        turn((0, 1))
-        quantise_rates((6, 7))
-        flux((6, 7))
-        damp_substrate(2, False)
+        turn((0, 1), 1)
         damp_substrate(3, False)
-        rate(2)
-        turn((2,))
+        quantise_rates((6, 7))
+        flux((6, 7), 0, 4)
+        rate(2, (6, 7))
+        turn((2,), 3)
         rate(3)
-        turn((3,), True)
+        turn((3,), 0, True)
+        flux((6, 7), 2, 5)
         quantise_rates((0, 1))
-        flux((0, 1))
+        flux((0, 1), 0, 7)
+        flux((0, 1), 2, 6, True)
         quantise_rates((2,))
-        flux((2,), True)
+        flux((2,), 0, 2)
+        flux((2,), 2, 4, True)
         quantise_rates((3,))
-        flux((3,), True)
+        flux((3,), 0, 1)
+        flux((3,), 2, 3, True)

@@ -24,7 +24,13 @@ CHUNK = 512
 BLOCK = 128
 CHUNKS = S // CHUNK
 BLOCKS = S // BLOCK
-PER = CHUNK // BLOCK
+PER_CHUNK = CHUNK // BLOCK
+PASS_GAP = 16
+
+LATE_WORDS_AT = 0
+LATE_DAMPING_AT = 6144
+PLACES_AT = 12288
+PLACE_BYTES = 4096
 
 
 def tile_list_inhibited_enzyme_fluxes_kernel(
@@ -47,9 +53,9 @@ def tile_list_inhibited_enzyme_fluxes_kernel(
         wi_sc = keep.tile([P, PASSES, H // 4], I32, align_bytes=64)
         ws_sc = keep.tile([P, PASSES, H // 4], I32, align_bytes=64)
         st_sc = keep.tile([P, N // 4], I32, align_bytes=64)
-        we_raw = [keep.tile([P, 4, H], F32, name="we_raw%d" % a, tag="we_raw%d" % a) for a in range(PASSES)]
+        we_raw = [keep.tile([P, 4, H], F32, name="we_raw%d" % a) for a in range(PASSES)]
         bias = keep.tile([P, N // P], F32)
-        shifted = {name: keep.tile([P, S // 4], I32, name="shifted_" + name, align_bytes=64) for name in "iec"}
+        second_plane = {name: keep.tile([P, S // 4], I32, name="second_plane_" + name, align_bytes=64) for name in "iec"}
         ident = keep.tile([P, P], F32)
         warm_in = keep.tile([P, 1], F32)
         warm_out = keep.tile([P, 1], F32)
@@ -61,19 +67,12 @@ def tile_list_inhibited_enzyme_fluxes_kernel(
         nc.vector.memset(ws_sc[:], 0)
         nc.vector.memset(st_sc[:], 0)
         for name in "iec":
-            nc.vector.memset(shifted[name][:], 0)
+            nc.vector.memset(second_plane[name][:], 0)
         nc.vector.memset(ident[:], 0.0)
         make_identity(nc, ident[:], nomemset=True)
 
         def load_tab(a):
             nc.sync.dma_start(tab_w[a][:], tab_words[a].rearrange("p t i -> p (t i)").bitcast(I32))
-
-        nc.sync.dma_start(lists["i"][:], offs3)
-        nc.sync.dma_start(wi_w[:], wi8_words.rearrange("a p y i -> p a (y i)").bitcast(I32))
-        nc.sync.dma_start(lists["c"][:], offs2)
-        tab_sc_hbm = tab_scales.bitcast(I32)
-        for r in range(4):
-            nc.sync.dma_start(tab_sc[r:P:16, :], tab_sc_hbm[:, r:16:4, :].rearrange("a q n -> q a n"))
 
         def load_planes(tile, scales):
             hbm = scales.bitcast(I32)
@@ -83,6 +82,12 @@ def tile_list_inhibited_enzyme_fluxes_kernel(
         def load_we(a):
             nc.sync.dma_start(we_raw[a][:], we[512 * a : 512 * (a + 1), :].rearrange("(p j) r -> p j r", j=4))
 
+        nc.sync.dma_start(lists["i"][:], offs3)
+        nc.sync.dma_start(wi_w[:], wi8_words.rearrange("a p y i -> p a (y i)").bitcast(I32))
+        nc.sync.dma_start(lists["c"][:], offs2)
+        tab_sc_hbm = tab_scales.bitcast(I32)
+        for r in range(4):
+            nc.sync.dma_start(tab_sc[r:P:PASS_GAP, :], tab_sc_hbm[:, r:16:4, :].rearrange("a q n -> q a n"))
         load_tab(0)
         load_planes(wi_sc, wi8_scales)
         load_tab(1)
@@ -101,9 +106,9 @@ def tile_list_inhibited_enzyme_fluxes_kernel(
         picked_sc = {name: keep.tile([P, S], U8, name="picked_sc_" + name, align_bytes=64) for name in "iec"}
         picked_w = {}
 
-        def gather_scales(name):
+        def gather_scales(name, queue):
             nc.vector.tensor_copy(picked_sc[name][:], tab_sc[:].bitcast(U8).indirect(lists[name][:]))
-            (nc.sync if name == "e" else nc.gpsimd).dma_start(shifted[name][0 : P - 16, :], picked_sc[name][16:P, :].bitcast(I32))
+            queue.dma_start(second_plane[name][0 : P - PASS_GAP, :], picked_sc[name][PASS_GAP:P, :].bitcast(I32))
 
         def gather_words(name, a, ch, into=None):
             cols = slice(ch * CHUNK // 16, (ch + 1) * CHUNK // 16)
@@ -112,31 +117,27 @@ def tile_list_inhibited_enzyme_fluxes_kernel(
             picked_w[name, a, ch] = into
             nc.vector.tensor_copy(into, tab_w[a][:].bitcast(U32).indirect(lists[name][:, cols]))
 
+        we_bf = reused.tile([P, PASSES, H, 4], BF16, offset=0, align_bytes=64)
         we_w = keep.tile([P, PASSES, H], U32, align_bytes=64)
         we_sc = keep.tile([P, PASSES, H], U8, align_bytes=64)
 
         def round_we(a):
             nc.gpsimd.tensor_scalar(we_bf[:, a], we_raw[a][:].rearrange("p j r -> p r j"), 1.0, 0.0, MULT, ADD)
 
-        def quantise_we():
-            nc.vector.quantize_mx(out=we_w[:].rearrange("p a r -> p (a r)").bitcast(FP8X4),
-                                  scales=we_sc[:].rearrange("p a r -> p (a r)"),
-                                  in_=we_bf[:].rearrange("p a r j -> p (a r j)"))
-
         def take_bank(bank, shape):
             return psum.tile([P] + shape, F32, name="bank%d" % bank, tag="bank%d" % bank)
 
+        accumulators = {}
         sums = {}
-        banks = {}
 
         def multiply(name, blk, bank, passes=range(PASSES)):
-            ch, cols = blk // PER, slice((blk % PER) * BLOCK, (blk % PER + 1) * BLOCK)
-            all_cols = slice(blk * BLOCK, (blk + 1) * BLOCK)
+            ch, cols = blk // PER_CHUNK, slice((blk % PER_CHUNK) * BLOCK, (blk % PER_CHUNK + 1) * BLOCK)
+            entries = slice(blk * BLOCK, (blk + 1) * BLOCK)
             if 0 in passes:
-                banks[name, blk] = take_bank(bank, [H])
-            acc = banks[name, blk]
+                accumulators[name, blk] = take_bank(bank, [H])
+            acc = accumulators[name, blk]
             for a in passes:
-                plane = picked_sc[name][:, all_cols] if a == 0 else shifted[name][:].bitcast(U8)[:, all_cols]
+                plane = picked_sc[name][:, entries] if a == 0 else second_plane[name][:].bitcast(U8)[:, entries]
                 if name == "c":
                     rhs = ws_w[:, a, :].bitcast(U8).bitcast(FP4X4)
                     rhs_scale = ws_sc[:, a, :].bitcast(U8)
@@ -145,11 +146,13 @@ def tile_list_inhibited_enzyme_fluxes_kernel(
                     rhs_scale = wi_sc[:, a, :].bitcast(U8) if name == "i" else we_sc[:, a, :]
                 nc.tensor.matmul_mx(out=acc[:], lhsT=picked_w[name, a, ch][:, cols].bitcast(FP8X4), lhsT_scale=plane,
                                     rhs=rhs, rhs_scale=rhs_scale, start=(a == 0), stop=(a == PASSES - 1))
-            sums[name, blk] = acc[:].rearrange("p (m u e) -> p u m e", u=2, e=2)
+            sums[name, blk] = acc[:].rearrange("p (m u z) -> p u m z", u=2, z=2)
 
         def as_pairs(tile):
-            return tile[:, :].rearrange("p (u m e) -> p u m e", u=2, e=2)
+            return tile[:, :].rearrange("p (u m z) -> p u m z", u=2, z=2)
 
+        squares = [keep.tile([P, 2, H], F32, name="squares%d" % pair) for pair in range(BLOCKS // 2)]
+        roots = [keep.tile([P, 2, H], F32, name="roots%d" % pair) for pair in range(BLOCKS // 2)]
         damp = {}
         levels = {}
         damped = {}
@@ -158,42 +161,43 @@ def tile_list_inhibited_enzyme_fluxes_kernel(
         place = {}
         h_mx = {}
 
-        squares = [keep.tile([P, 2, H], F32, name="squares%d" % pair) for pair in range(BLOCKS // 2)]
-        roots = [keep.tile([P, 2, H], F32, name="roots%d" % pair) for pair in range(BLOCKS // 2)]
-
         def square_inhibitor(blk):
             nc.scalar.activation(as_pairs(squares[blk // 2][:, blk % 2, :]), sums["i", blk], ACT.Square)
 
         def inverse_root(first):
             nc.scalar.activation(roots[first // 2][:], squares[first // 2][:], ACT.Abs_reciprocal_sqrt, bias=1.0)
 
-        def damping(first, count, into=None):
-            root = roots[first // 2][:, first % 2 : first % 2 + count, :]
-            if into is None:
-                into = keep.tile([P, count, H], F32, name="damp%d" % first)[:]
-                nc.scalar.activation(into, root, ACT.Square)
+        def damping(first, on_gpsimd=False):
+            root = roots[first // 2][:]
+            if on_gpsimd:
+                into = reused.tile([P, 2, H], F32, name="damp%d" % first, offset=LATE_DAMPING_AT, align_bytes=64)
+                nc.gpsimd.tensor_tensor(into[:], root, root, MULT)
             else:
-                nc.gpsimd.tensor_tensor(into, root, root, MULT)
-            for g in range(count):
+                into = keep.tile([P, 2, H], F32, name="damp%d" % first)
+                nc.scalar.activation(into[:], root, ACT.Square)
+            for g in range(2):
                 damp[first + g] = into[:, g, :]
 
         def copy_substrate(blk):
             levels[blk] = ring.tile([P, H], F32, name="level")
             nc.scalar.copy(as_pairs(levels[blk]), sums["c", blk])
 
-        def damp_substrate(blk, on_gpsimd):
-            damped[blk] = ring.tile([P, H], F32, name="damped", bufs=BLOCKS)[:]
-            if on_gpsimd:
-                nc.gpsimd.tensor_tensor(damped[blk], levels[blk][:], damp[blk], MULT)
+        def damp_substrate(blk, behind=None):
+            if behind is None:
+                damped[blk] = ring.tile([P, H], F32, name="damped", bufs=BLOCKS)
             else:
-                nc.vector.tensor_tensor(as_pairs(damped[blk]), sums["c", blk], as_pairs(damp[blk]), MULT)
+                damped[blk] = reused.tile([P, H], F32, name="damped%d" % blk, offset=place[behind] + 2 * H, align_bytes=64)
+            if blk in levels:
+                nc.gpsimd.tensor_tensor(damped[blk][:], levels[blk][:], damp[blk], MULT)
+            else:
+                nc.vector.tensor_tensor(as_pairs(damped[blk]), as_pairs(damp[blk]), sums["c", blk], MULT)
 
         def rate(blk, behind=None):
             if behind is None:
                 rates[blk] = ring.tile([P, H], BF16, name="rate", align_bytes=64)
             else:
                 rates[blk] = reused.tile([P, H], BF16, name="rate%d" % blk, offset=place[behind], align_bytes=64)
-            nc.vector.tensor_tensor(as_pairs(rates[blk]), sums["e", blk], as_pairs(damped[blk]), MULT)
+            nc.vector.tensor_tensor(as_pairs(rates[blk]), as_pairs(damped[blk]), sums["e", blk], MULT)
 
         def turn(group, bank, on_vector=False):
             turned = take_bank(bank, [len(group), 2, BLOCK])
@@ -201,12 +205,11 @@ def tile_list_inhibited_enzyme_fluxes_kernel(
                 words = rates[blk][:].bitcast(F32)
                 for u in range(2):
                     nc.tensor.transpose(turned[:, g, u, :], words[:, u * P : (u + 1) * P], ident[:])
-            place[group] = 12288 + 2048 * len(place)
-            grouped[group] = reused.tile([P, len(group), BLOCK, 4], BF16, name="grouped%d" % group[0], offset=place[group], align_bytes=64)
-            if on_vector:
-                nc.vector.tensor_copy(grouped[group][:].bitcast(F32), turned[:].rearrange("p g u j -> p g j u"))
-            else:
-                nc.scalar.copy(grouped[group][:].bitcast(F32), turned[:].rearrange("p g u j -> p g j u"))
+            place[group] = PLACES_AT + PLACE_BYTES * len(place)
+            grouped[group] = reused.tile([P, len(group), BLOCK, 4], BF16, name="grouped%d" % group[0],
+                                         offset=place[group], align_bytes=64)
+            copy = nc.vector.tensor_copy if on_vector else nc.scalar.copy
+            copy(grouped[group][:].bitcast(F32), turned[:].rearrange("p g u j -> p g j u"))
 
         def quantise_rates(group):
             h_w = ring.tile([P, len(group) * BLOCK], U32, align_bytes=64)
@@ -227,89 +230,87 @@ def tile_list_inhibited_enzyme_fluxes_kernel(
                                     lhsT_scale=st_plane[:, P * c : P * (c + 1)],
                                     rhs=h_w[:].bitcast(FP8X4), rhs_scale=h_sc[:], start=True, stop=True)
             if on_vector:
-                nc.vector.tensor_tensor(result[:], y[:], bias[:, first : first + 2].unsqueeze(2).to_broadcast([P, 2, width]), ADD)
+                spread = bias[:, first : first + 2].unsqueeze(2).to_broadcast([P, 2, width])
+                nc.vector.tensor_tensor(result[:], spread, y[:], ADD)
             else:
                 for c in range(first, first + 2):
                     nc.scalar.activation(result[:, c - first, :], y[:, c - first, :], ACT.Identity, bias=bias[:, c : c + 1])
             rows = out[first * P : (first + 2) * P, group[0] * BLOCK : group[0] * BLOCK + width]
             nc.sync.dma_start(rows.rearrange("(c p) j -> p c j", p=P), result[:])
 
-        gather_scales("i")
-        gather_scales("c")
+        gather_scales("i", nc.gpsimd)
+        gather_scales("c", nc.gpsimd)
         for a in range(PASSES):
             for name in "ic":
                 for ch in range(CHUNKS):
                     gather_words(name, a, ch)
             for blk in range(BLOCKS):
                 multiply("i", blk, blk, [a])
-        gather_scales("e")
-        gather_words("e", 0, 1)
+        gather_scales("e", nc.sync)
+        for a in range(PASSES):
+            gather_words("e", a, 1)
         for blk in range(BLOCKS):
             square_inhibitor(blk)
-        we_bf = reused.tile([P, PASSES, H, 4], BF16, offset=0, align_bytes=64)
-        round_we(0)
-        round_we(1)
-        quantise_we()
-        late_words = reused.tile([P, 3, CHUNK], U32, offset=0, align_bytes=64)
-        late_pair = reused.tile([P, 2, H], F32, offset=6144, align_bytes=64)
-        gather_words("e", 1, 1, late_words[:, 0, :])
-        gather_words("e", 0, 0, late_words[:, 1, :])
-        gather_words("e", 1, 0, late_words[:, 2, :])
+        for a in range(PASSES):
+            round_we(a)
+        nc.vector.quantize_mx(out=we_w[:].rearrange("p a r -> p (a r)").bitcast(FP8X4),
+                              scales=we_sc[:].rearrange("p a r -> p (a r)"),
+                              in_=we_bf[:].rearrange("p a r j -> p (a r j)"))
+        late_words = reused.tile([P, PASSES, CHUNK], U32, offset=LATE_WORDS_AT, align_bytes=64)
+        for a in range(PASSES):
+            gather_words("e", a, 0, late_words[:, a, :])
+
         for bank, blk in enumerate((0, 1, 4, 2, 5, 6, 7, 3)):
             multiply("c", blk, bank)
         inverse_root(0)
-        damping(0, 2, late_pair[:])
-        copy_substrate(0)
-        damp_substrate(0, True)
-        multiply("e", 4, 0)
-        copy_substrate(1)
-        damp_substrate(1, True)
-        multiply("e", 5, 1)
+        damping(0, on_gpsimd=True)
         inverse_root(4)
+        copy_substrate(0)
+        damp_substrate(0)
+        multiply("e", 4, 0)
+        damping(4)
+        copy_substrate(1)
+        damp_substrate(1)
+        multiply("e", 5, 1)
+        inverse_root(6)
         copy_substrate(2)
         multiply("e", 6, 3)
+        damping(6)
         inverse_root(2)
-        damping(2, 1, reused.tile([P, 1, H], F32, name="late_single", offset=6144, align_bytes=64)[:])
-        damp_substrate(2, True)
-        damping(4, 2)
-        inverse_root(6)
-        damping(6, 2)
-        damp_substrate(4, False)
+
+        damp_substrate(4)
         multiply("e", 7, 2)
-        damp_substrate(5, False)
+        damp_substrate(5)
         multiply("e", 0, 4)
         rate(4)
         rate(5)
         turn((4, 5), 0)
         multiply("e", 1, 1)
-        damping(3, 1)
-        damp_substrate(6, False)
+        damping(2)
+        damp_substrate(6)
         rate(6)
         multiply("e", 2, 3)
-        damp_substrate(7, False)
+        damp_substrate(7)
         quantise_rates((4, 5))
+        damp_substrate(2, behind=(4, 5))
         flux((4, 5), 0, 5)
         multiply("e", 3, 0)
-        rate(7, (4, 5))
+        rate(7, behind=(4, 5))
         turn((6, 7), 2)
         flux((4, 5), 2, 6)
         rate(0)
         rate(1)
         turn((0, 1), 1)
-        damp_substrate(3, False)
+        damp_substrate(3)
         quantise_rates((6, 7))
         flux((6, 7), 0, 4)
-        rate(2, (6, 7))
+        rate(2, behind=(6, 7))
+
         turn((2,), 3)
         rate(3)
-        turn((3,), 0, True)
+        turn((3,), 0, on_vector=True)
         flux((6, 7), 2, 5)
-        quantise_rates((0, 1))
-        flux((0, 1), 0, 7)
-        flux((0, 1), 2, 6, True)
-        quantise_rates((2,))
-        flux((2,), 0, 2)
-        flux((2,), 2, 4, True)
-        quantise_rates((3,))
-        flux((3,), 0, 1)
-        flux((3,), 2, 3, True)
+        for group, banks in (((0, 1), (7, 6)), ((2,), (2, 4)), ((3,), (1, 3))):
+            quantise_rates(group)
+            flux(group, 0, banks[0])
+            flux(group, 2, banks[1], on_vector=True)

@@ -1,7 +1,6 @@
 from contextlib import ExitStack
 
 import concourse.mybir as mybir
-from concourse.masks import make_identity
 
 K, T, S, H, N = 1024, 4096, 1024, 512, 512
 FLOPS = 2 * S * (3 * K * H + H * N)
@@ -20,17 +19,18 @@ ADD = mybir.AluOpType.add
 
 P = 128
 PASSES = K // 512
+SLOTS = 4
 CHUNK = 512
 BLOCK = 128
 CHUNKS = S // CHUNK
 BLOCKS = S // BLOCK
-PER_CHUNK = CHUNK // BLOCK
 PASS_GAP = 16
 
-LATE_WORDS_AT = 0
-LATE_DAMPING_AT = 6144
-PLACES_AT = 12288
-PLACE_BYTES = 4096
+ROUNDED_WE_AT = 4096
+LATE_PAIRS_AT = {4: ROUNDED_WE_AT + 64 - 4096, 6: ROUNDED_WE_AT + 8192 - 64}
+LATE_WORDS_AT = ROUNDED_WE_AT + 64
+LATE_DAMPED_AT = LATE_WORDS_AT + 4096
+LAST_LEVEL_AT = 20480
 
 
 def tile_list_inhibited_enzyme_fluxes_kernel(
@@ -40,7 +40,6 @@ def tile_list_inhibited_enzyme_fluxes_kernel(
     nc = tc.nc
     with ExitStack() as ctx:
         keep = ctx.enter_context(tc.tile_pool(name="keep", bufs=1))
-        ring = ctx.enter_context(tc.tile_pool(name="ring", bufs=6))
         reused = ctx.enter_context(tc.tile_pool(name="reused", bufs=1))
         psum = ctx.enter_context(tc.psum_pool(name="psum", bufs=1))
 
@@ -53,10 +52,9 @@ def tile_list_inhibited_enzyme_fluxes_kernel(
         wi_sc = keep.tile([P, PASSES, H // 4], I32, align_bytes=64)
         ws_sc = keep.tile([P, PASSES, H // 4], I32, align_bytes=64)
         st_sc = keep.tile([P, N // 4], I32, align_bytes=64)
-        we_raw = [keep.tile([P, 4, H], F32, name="we_raw%d" % a) for a in range(PASSES)]
+        we_raw = [keep.tile([P, SLOTS, H // 2], F32, name="we_raw%d" % part) for part in range(4)]
         bias = keep.tile([P, N // P], F32)
         second_plane = {name: keep.tile([P, S // 4], I32, name="second_plane_" + name, align_bytes=64) for name in "iec"}
-        ident = keep.tile([P, P], F32)
         warm_in = keep.tile([P, 1], F32)
         warm_out = keep.tile([P, 1], F32)
 
@@ -68,19 +66,19 @@ def tile_list_inhibited_enzyme_fluxes_kernel(
         nc.vector.memset(st_sc[:], 0)
         for name in "iec":
             nc.vector.memset(second_plane[name][:], 0)
-        nc.vector.memset(ident[:], 0.0)
-        make_identity(nc, ident[:], nomemset=True)
 
         def load_tab(a):
             nc.sync.dma_start(tab_w[a][:], tab_words[a].rearrange("p t i -> p (t i)").bitcast(I32))
 
-        def load_planes(tile, scales):
+        def load_planes(tile, scales, queue):
             hbm = scales.bitcast(I32)
             for r in range(4):
-                nc.sync.dma_start(tile[r:P:32, :, :], hbm[:, r:16:4, :].rearrange("a q n -> q a n"))
+                queue.dma_start(tile[r:P:32, :, :], hbm[:, r:16:4, :].rearrange("a q n -> q a n"))
 
-        def load_we(a):
-            nc.sync.dma_start(we_raw[a][:], we[512 * a : 512 * (a + 1), :].rearrange("(p j) r -> p j r", j=4))
+        def load_we(part):
+            a, half = divmod(part, 2)
+            rows = we[512 * a : 512 * (a + 1), half * H // 2 : (half + 1) * H // 2]
+            nc.sync.dma_start(we_raw[part][:], rows.rearrange("(p j) r -> p j r", j=SLOTS))
 
         nc.sync.dma_start(lists["i"][:], offs3)
         nc.sync.dma_start(wi_w[:], wi8_words.rearrange("a p y i -> p a (y i)").bitcast(I32))
@@ -89,19 +87,27 @@ def tile_list_inhibited_enzyme_fluxes_kernel(
         for r in range(4):
             nc.sync.dma_start(tab_sc[r:P:PASS_GAP, :], tab_sc_hbm[:, r:16:4, :].rearrange("a q n -> q a n"))
         load_tab(0)
-        load_planes(wi_sc, wi8_scales)
+        load_planes(wi_sc, wi8_scales, nc.sync)
+        nc.sync.dma_start(ws_w[:], ws4_words.rearrange("a p y -> p a y").bitcast(I32))
         load_tab(1)
         nc.sync.dma_start(lists["e"][:], offs)
-        load_we(0)
-        nc.sync.dma_start(ws_w[:], ws4_words.rearrange("a p y -> p a y").bitcast(I32))
-        load_planes(ws_sc, ws4_scales)
-        load_we(1)
+        load_planes(ws_sc, ws4_scales, nc.sync)
+        for part in range(4):
+            load_we(part)
         nc.sync.dma_start(st_w[:], st4_words[0].bitcast(I32))
         with nc.allow_non_contiguous_dma(reason="one bias value a partition"):
             nc.sync.dma_start(bias[:], b.rearrange("(c p) -> p c", p=P))
         st_sc_hbm = st4_scales.bitcast(I32)
         for r in range(4):
             nc.sync.dma_start(st_sc[r:P:32, :], st_sc_hbm[0, r:16:4, :])
+
+        wi_dealt = keep.tile([P, SLOTS, PASSES * BLOCK], I32, align_bytes=64)
+        ws_dealt = keep.tile([P, SLOTS, PASSES * BLOCK, 2], U8, align_bytes=64)
+        wi_sc_dealt = keep.tile([P, SLOTS, PASSES * BLOCK], U8, align_bytes=64)
+        ws_sc_dealt = keep.tile([P, SLOTS, PASSES * BLOCK], U8, align_bytes=64)
+
+        def deal_plane(into, plane):
+            nc.gpsimd.tensor_copy(into[:], plane[:].rearrange("p a y -> p (a y)").bitcast(U8).rearrange("p (m t) -> p t m", t=SLOTS))
 
         picked_sc = {name: keep.tile([P, S], U8, name="picked_sc_" + name, align_bytes=64) for name in "iec"}
         picked_w = {}
@@ -117,105 +123,113 @@ def tile_list_inhibited_enzyme_fluxes_kernel(
             picked_w[name, a, ch] = into
             nc.vector.tensor_copy(into, tab_w[a][:].bitcast(U32).indirect(lists[name][:, cols]))
 
-        we_bf = reused.tile([P, PASSES, H, 4], BF16, offset=0, align_bytes=64)
-        we_w = keep.tile([P, PASSES, H], U32, align_bytes=64)
-        we_sc = keep.tile([P, PASSES, H], U8, align_bytes=64)
+        we_bf = reused.tile([P, PASSES, SLOTS, BLOCK, SLOTS], BF16, offset=ROUNDED_WE_AT, align_bytes=64)
+        we_w = keep.tile([P, PASSES, SLOTS, BLOCK], U32, align_bytes=64)
+        we_sc = keep.tile([P, PASSES, SLOTS, BLOCK], U8, align_bytes=64)
 
-        def round_we(a):
-            nc.gpsimd.tensor_scalar(we_bf[:, a], we_raw[a][:].rearrange("p j r -> p r j"), 1.0, 0.0, MULT, ADD)
+        def round_we(part):
+            a, half = divmod(part, 2)
+            into = we_bf[:, a, :, half * BLOCK // 2 : (half + 1) * BLOCK // 2, :]
+            nc.gpsimd.tensor_scalar(into.rearrange("p t m j -> p m t j"),
+                                    we_raw[part][:].rearrange("p j (m t) -> p m t j", t=SLOTS), 1.0, 0.0, MULT, ADD)
 
         def take_bank(bank, shape):
             return psum.tile([P] + shape, F32, name="bank%d" % bank, tag="bank%d" % bank)
 
+        def stationary(name, a, t):
+            cols = slice(a * BLOCK, (a + 1) * BLOCK)
+            if name == "i":
+                return wi_dealt[:, t, cols].bitcast(FP8X4), wi_sc_dealt[:, t, cols]
+            if name == "e":
+                return we_w[:, a, t, :].bitcast(FP8X4), we_sc[:, a, t, :]
+            return ws_dealt[:, t, cols, :].rearrange("p m h -> p (m h)").bitcast(FP4X4), ws_sc_dealt[:, t, cols]
+
         accumulators = {}
         sums = {}
 
-        def multiply(name, blk, bank, passes=range(PASSES)):
-            ch, cols = blk // PER_CHUNK, slice((blk % PER_CHUNK) * BLOCK, (blk % PER_CHUNK + 1) * BLOCK)
+        def one_pass(name, blk, a, t, start, stop):
+            ch = blk * BLOCK // CHUNK
+            cols = slice(blk * BLOCK % CHUNK, blk * BLOCK % CHUNK + BLOCK)
             entries = slice(blk * BLOCK, (blk + 1) * BLOCK)
-            if 0 in passes:
-                accumulators[name, blk] = take_bank(bank, [H])
-            acc = accumulators[name, blk]
-            for a in passes:
-                plane = picked_sc[name][:, entries] if a == 0 else second_plane[name][:].bitcast(U8)[:, entries]
-                if name == "c":
-                    rhs = ws_w[:, a, :].bitcast(U8).bitcast(FP4X4)
-                    rhs_scale = ws_sc[:, a, :].bitcast(U8)
-                else:
-                    rhs = (wi_w if name == "i" else we_w)[:, a, :].bitcast(FP8X4)
-                    rhs_scale = wi_sc[:, a, :].bitcast(U8) if name == "i" else we_sc[:, a, :]
-                nc.tensor.matmul_mx(out=acc[:], lhsT=picked_w[name, a, ch][:, cols].bitcast(FP8X4), lhsT_scale=plane,
-                                    rhs=rhs, rhs_scale=rhs_scale, start=(a == 0), stop=(a == PASSES - 1))
-            sums[name, blk] = acc[:].rearrange("p (m u z) -> p u m z", u=2, z=2)
+            plane = picked_sc[name][:, entries] if a == 0 else second_plane[name][:].bitcast(U8)[:, entries]
+            lhsT, lhsT_scale = stationary(name, a, t)
+            nc.tensor.matmul_mx(out=accumulators[name, blk][:, t, :], lhsT=lhsT, lhsT_scale=lhsT_scale,
+                                rhs=picked_w[name, a, ch][:, cols].bitcast(FP8X4), rhs_scale=plane, start=start, stop=stop)
 
-        def as_pairs(tile):
-            return tile[:, :].rearrange("p (u m z) -> p u m z", u=2, z=2)
+        def multiply(name, blk, bank):
+            accumulators[name, blk] = take_bank(bank, [SLOTS, BLOCK])
+            for t in range(SLOTS):
+                for a in range(PASSES):
+                    one_pass(name, blk, a, t, a == 0, a == PASSES - 1)
+            sums[name, blk] = accumulators[name, blk][:].rearrange("p t j -> p j t")
+
+        def multiply_pass(name, blk, bank, a):
+            if a == 0:
+                accumulators[name, blk] = take_bank(bank, [SLOTS, BLOCK])
+            for t in range(SLOTS):
+                one_pass(name, blk, a, t, a == 0 and t == 0, a == PASSES - 1 and t == SLOTS - 1)
+            sums[name, blk] = accumulators[name, blk][:].rearrange("p t j -> p j t")
+
+        def woven(ap):
+            return ap.rearrange("p (j t) -> p j t", t=SLOTS)
 
         squares = [keep.tile([P, 2, H], F32, name="squares%d" % pair) for pair in range(BLOCKS // 2)]
         roots = [keep.tile([P, 2, H], F32, name="roots%d" % pair) for pair in range(BLOCKS // 2)]
+        rates = [keep.tile([P, 2, H], BF16, name="rates%d" % pair, align_bytes=64) for pair in range(BLOCKS // 2)]
         damp = {}
         levels = {}
         damped = {}
-        rates = {}
-        grouped = {}
-        place = {}
         h_mx = {}
 
         def square_inhibitor(blk):
-            nc.scalar.activation(as_pairs(squares[blk // 2][:, blk % 2, :]), sums["i", blk], ACT.Square)
+            nc.scalar.activation(woven(squares[blk // 2][:, blk % 2, :]), sums["i", blk], ACT.Square)
 
         def inverse_root(first):
             nc.scalar.activation(roots[first // 2][:], squares[first // 2][:], ACT.Abs_reciprocal_sqrt, bias=1.0)
 
         def damping(first, on_gpsimd=False):
             root = roots[first // 2][:]
+            into = keep.tile([P, 2, H], F32, name="damp%d" % first)
             if on_gpsimd:
-                into = reused.tile([P, 2, H], F32, name="damp%d" % first, offset=LATE_DAMPING_AT, align_bytes=64)
                 nc.gpsimd.tensor_tensor(into[:], root, root, MULT)
             else:
-                into = keep.tile([P, 2, H], F32, name="damp%d" % first)
                 nc.scalar.activation(into[:], root, ACT.Square)
             for g in range(2):
                 damp[first + g] = into[:, g, :]
 
-        def copy_substrate(blk):
-            levels[blk] = ring.tile([P, H], F32, name="level")
-            nc.scalar.copy(as_pairs(levels[blk]), sums["c", blk])
-
-        def damp_substrate(blk, behind=None):
-            if behind is None:
-                damped[blk] = ring.tile([P, H], F32, name="damped", bufs=BLOCKS)
+        def copy_substrate(blk, at=None):
+            if at is None:
+                levels[blk] = keep.tile([P, H], F32, name="level%d" % blk)
             else:
-                damped[blk] = reused.tile([P, H], F32, name="damped%d" % blk, offset=place[behind] + 2 * H, align_bytes=64)
+                levels[blk] = reused.tile([P, H], F32, name="level%d" % blk, offset=at, align_bytes=64)
+            nc.scalar.copy(woven(levels[blk][:]), sums["c", blk])
+
+        def damp_substrate(blk, at=None):
+            if blk in LATE_PAIRS_AT:
+                pair = reused.tile([P, 2, H], F32, name="damped%d" % blk, offset=LATE_PAIRS_AT[blk], align_bytes=64)
+                damped[blk], damped[blk + 1] = pair[:, 0, :], pair[:, 1, :]
+            elif at is not None:
+                damped[blk] = reused.tile([P, H], F32, name="damped%d" % blk, offset=at, align_bytes=64)[:]
+            elif blk not in damped:
+                damped[blk] = keep.tile([P, H], F32, name="damped%d" % blk)[:]
             if blk in levels:
-                nc.gpsimd.tensor_tensor(damped[blk][:], levels[blk][:], damp[blk], MULT)
+                nc.gpsimd.tensor_tensor(damped[blk], levels[blk][:], damp[blk], MULT)
             else:
-                nc.vector.tensor_tensor(as_pairs(damped[blk]), as_pairs(damp[blk]), sums["c", blk], MULT)
+                nc.vector.tensor_tensor(woven(damped[blk]), woven(damp[blk]), sums["c", blk], MULT)
 
-        def rate(blk, behind=None):
-            if behind is None:
-                rates[blk] = ring.tile([P, H], BF16, name="rate", align_bytes=64)
+        def rate(blk):
+            nc.vector.tensor_tensor(woven(rates[blk // 2][:, blk % 2, :]), woven(damped[blk]), sums["e", blk], MULT)
+
+        def quantise_rates(group, at=None):
+            width = len(group) * BLOCK
+            if at is None:
+                h_w = keep.tile([P, width], U32, name="h_w%d" % group[0], align_bytes=64)
             else:
-                rates[blk] = reused.tile([P, H], BF16, name="rate%d" % blk, offset=place[behind], align_bytes=64)
-            nc.vector.tensor_tensor(as_pairs(rates[blk]), as_pairs(damped[blk]), sums["e", blk], MULT)
-
-        def turn(group, bank, on_vector=False):
-            turned = take_bank(bank, [len(group), 2, BLOCK])
-            for g, blk in enumerate(group):
-                words = rates[blk][:].bitcast(F32)
-                for u in range(2):
-                    nc.tensor.transpose(turned[:, g, u, :], words[:, u * P : (u + 1) * P], ident[:])
-            place[group] = PLACES_AT + PLACE_BYTES * len(place)
-            grouped[group] = reused.tile([P, len(group), BLOCK, 4], BF16, name="grouped%d" % group[0],
-                                         offset=place[group], align_bytes=64)
-            copy = nc.vector.tensor_copy if on_vector else nc.scalar.copy
-            copy(grouped[group][:].bitcast(F32), turned[:].rearrange("p g u j -> p g j u"))
-
-        def quantise_rates(group):
-            h_w = ring.tile([P, len(group) * BLOCK], U32, align_bytes=64)
-            h_sc = ring.tile([P, len(group) * BLOCK], U8, align_bytes=64)
+                h_w = reused.tile([P, width], U32, name="h_w%d" % group[0], offset=at, align_bytes=64)
+            h_sc = keep.tile([P, width], U8, name="h_sc%d" % group[0], align_bytes=64)
+            first = group[0] % 2
             nc.vector.quantize_mx(out=h_w[:].bitcast(FP8X4), scales=h_sc[:],
-                                  in_=grouped[group][:].rearrange("p g j t -> p (g j t)"))
+                                  in_=rates[group[0] // 2][:, first : first + len(group), :].rearrange("p g x -> p (g x)"))
             h_mx[group] = h_w, h_sc
 
         def flux(group, first, bank, on_vector=False):
@@ -223,7 +237,7 @@ def tile_list_inhibited_enzyme_fluxes_kernel(
             width = len(group) * BLOCK
             st_bytes = st_w[:].bitcast(U8)
             st_plane = st_sc[:].bitcast(U8)
-            result = ring.tile([P, 2, width], F32, bufs=10)
+            result = keep.tile([P, 2, width], F32, name="result%d_%d" % (group[0], first))
             y = take_bank(bank, [2, width])
             for c in range(first, first + 2):
                 nc.tensor.matmul_mx(out=y[:, c - first, :], lhsT=st_bytes[:, 2 * P * c : 2 * P * (c + 1)].bitcast(FP4X4),
@@ -238,79 +252,79 @@ def tile_list_inhibited_enzyme_fluxes_kernel(
             rows = out[first * P : (first + 2) * P, group[0] * BLOCK : group[0] * BLOCK + width]
             nc.sync.dma_start(rows.rearrange("(c p) j -> p c j", p=P), result[:])
 
+        nc.gpsimd.tensor_copy(wi_dealt[:].rearrange("p t (g i) -> p g t i", i=4),
+                              wi_w[:].rearrange("p a (g i t) -> p (a g) t i", i=4, t=SLOTS))
         gather_scales("i", nc.gpsimd)
         gather_scales("c", nc.gpsimd)
+        deal_plane(wi_sc_dealt, wi_sc)
+        nc.gpsimd.tensor_copy(ws_dealt[:], ws_w[:].rearrange("p a y -> p (a y)").bitcast(U8).rearrange("p (m t h) -> p t m h", t=SLOTS, h=2))
+        deal_plane(ws_sc_dealt, ws_sc)
         for a in range(PASSES):
-            for name in "ic":
-                for ch in range(CHUNKS):
+            for ch in range(CHUNKS):
+                for name in "ic":
                     gather_words(name, a, ch)
-            for blk in range(BLOCKS):
-                multiply("i", blk, blk, [a])
+            for blk in range(4):
+                multiply_pass("i", blk, blk, a)
         gather_scales("e", nc.sync)
         for a in range(PASSES):
-            gather_words("e", a, 1)
-        for blk in range(BLOCKS):
-            square_inhibitor(blk)
-        for a in range(PASSES):
-            round_we(a)
-        nc.vector.quantize_mx(out=we_w[:].rearrange("p a r -> p (a r)").bitcast(FP8X4),
-                              scales=we_sc[:].rearrange("p a r -> p (a r)"),
-                              in_=we_bf[:].rearrange("p a r j -> p (a r j)"))
+            gather_words("e", a, 0)
+        for part in range(4):
+            round_we(part)
+        nc.vector.quantize_mx(out=we_w[:].rearrange("p a t m -> p (a t m)").bitcast(FP8X4),
+                              scales=we_sc[:].rearrange("p a t m -> p (a t m)"),
+                              in_=we_bf[:].rearrange("p a t m j -> p (a t m j)"))
         late_words = reused.tile([P, PASSES, CHUNK], U32, offset=LATE_WORDS_AT, align_bytes=64)
         for a in range(PASSES):
-            gather_words("e", a, 0, late_words[:, a, :])
+            gather_words("e", a, 1, late_words[:, a, :])
 
-        for bank, blk in enumerate((0, 1, 4, 2, 5, 6, 7, 3)):
-            multiply("c", blk, bank)
+        for blk in range(4):
+            multiply("c", blk, 4 + blk)
+        square_inhibitor(0)
+        square_inhibitor(1)
         inverse_root(0)
-        damping(0, on_gpsimd=True)
-        inverse_root(4)
-        copy_substrate(0)
-        damp_substrate(0)
-        multiply("e", 4, 0)
-        damping(4)
-        copy_substrate(1)
-        damp_substrate(1)
-        multiply("e", 5, 1)
-        inverse_root(6)
-        copy_substrate(2)
-        multiply("e", 6, 3)
-        damping(6)
+        square_inhibitor(2)
+        square_inhibitor(3)
         inverse_root(2)
+        damping(2, on_gpsimd=True)
+        damping(0)
+        for blk in range(4):
+            copy_substrate(blk, LAST_LEVEL_AT if blk == 3 else None)
+            damp_substrate(blk, LATE_DAMPED_AT if blk == 0 else None)
+            multiply("i", 4 + blk, 4 + blk)
+        for blk in range(4, BLOCKS):
+            multiply("c", blk, blk - 4)
+        for first in (4, 6):
+            for blk in (first, first + 1):
+                square_inhibitor(blk)
+                multiply("e", blk - 4, blk)
+            inverse_root(first)
+            damping(first)
 
+        for blk in range(2):
+            rate(blk)
+            multiply("e", 4 + blk, 4 + blk)
         damp_substrate(4)
-        multiply("e", 7, 2)
         damp_substrate(5)
-        multiply("e", 0, 4)
+        quantise_rates((0, 1), LAST_LEVEL_AT)
+        flux((0, 1), 0, 0)
+        flux((0, 1), 2, 1)
         rate(4)
         rate(5)
-        turn((4, 5), 0)
-        multiply("e", 1, 1)
-        damping(2)
-        damp_substrate(6)
-        rate(6)
-        multiply("e", 2, 3)
-        damp_substrate(7)
+        rate(2)
+        multiply("e", 6, 6)
         quantise_rates((4, 5))
-        damp_substrate(2, behind=(4, 5))
-        flux((4, 5), 0, 5)
-        multiply("e", 3, 0)
-        rate(7, behind=(4, 5))
-        turn((6, 7), 2)
-        flux((4, 5), 2, 6)
-        rate(0)
-        rate(1)
-        turn((0, 1), 1)
-        damp_substrate(3)
-        quantise_rates((6, 7))
-        flux((6, 7), 0, 4)
-        rate(2, behind=(6, 7))
-
-        turn((2,), 3)
+        flux((4, 5), 0, 4)
+        flux((4, 5), 2, 5)
         rate(3)
-        turn((3,), 0, on_vector=True)
-        flux((6, 7), 2, 5)
-        for group, banks in (((0, 1), (7, 6)), ((2,), (2, 4)), ((3,), (1, 3))):
+        multiply("e", 7, 7)
+        damp_substrate(6)
+        quantise_rates((2, 3))
+        flux((2, 3), 0, 0)
+        flux((2, 3), 2, 1)
+        damp_substrate(7)
+        rate(6)
+        rate(7)
+        for group, banks in (((6,), (2, 3)), ((7,), (4, 5))):
             quantise_rates(group)
             flux(group, 0, banks[0])
             flux(group, 2, banks[1], on_vector=True)

@@ -27,9 +27,10 @@ BLOCKS = S // BLOCK
 PASS_GAP = 16
 
 ROUNDED_WE_AT = 4096
-LATE_PAIRS_AT = {4: ROUNDED_WE_AT + 64 - 4096, 6: ROUNDED_WE_AT + 8192 - 64}
-LATE_WORDS_AT = ROUNDED_WE_AT + 64
-LATE_DAMPED_AT = LATE_WORDS_AT + 4096
+SECOND_PASS_AT = 32768
+LATE_PAIRS_AT = {4: SECOND_PASS_AT, 6: SECOND_PASS_AT + 4096}
+LATE_WORDS_AT = ROUNDED_WE_AT + 64 - 4096
+LATE_DAMPED_AT = [ROUNDED_WE_AT + 64, ROUNDED_WE_AT + 64 + 2048, ROUNDED_WE_AT + 64 + 4096, ROUNDED_WE_AT + 8192 - 64]
 LAST_LEVEL_AT = 20480
 
 
@@ -45,7 +46,8 @@ def tile_list_inhibited_enzyme_fluxes_kernel(
 
         lists = {name: keep.tile([P, S // 16], U16, name="list_" + name) for name in "iec"}
         tab_sc = keep.tile([P, T // 4], I32, align_bytes=64)
-        tab_w = [keep.tile([P, T], I32, name="tab_w%d" % a, align_bytes=64) for a in range(PASSES)]
+        tab_w = [keep.tile([P, T], I32, name="tab_w0", align_bytes=64),
+                 reused.tile([P, T], I32, name="tab_w1", offset=SECOND_PASS_AT, align_bytes=64)]
         wi_w = keep.tile([P, PASSES, H], I32, align_bytes=64)
         ws_w = keep.tile([P, PASSES, H // 2], I32, align_bytes=64)
         st_w = keep.tile([P, N // 2], I32, align_bytes=64)
@@ -67,8 +69,9 @@ def tile_list_inhibited_enzyme_fluxes_kernel(
         for name in "iec":
             nc.vector.memset(second_plane[name][:], 0)
 
-        def load_tab(a):
-            nc.sync.dma_start(tab_w[a][:], tab_words[a].rearrange("p t i -> p (t i)").bitcast(I32))
+        def load_tab(a, half):
+            cols = slice(half * T // 2, (half + 1) * T // 2)
+            nc.sync.dma_start(tab_w[a][:, cols], tab_words[a].rearrange("p t i -> p (t i)").bitcast(I32)[:, cols])
 
         def load_planes(tile, scales, queue):
             hbm = scales.bitcast(I32)
@@ -80,19 +83,33 @@ def tile_list_inhibited_enzyme_fluxes_kernel(
             rows = we[512 * a : 512 * (a + 1), half * H // 2 : (half + 1) * H // 2]
             nc.sync.dma_start(we_raw[part][:], rows.rearrange("(p j) r -> p j r", j=SLOTS))
 
+        picked_sc = {name: keep.tile([P, S], U8, name="picked_sc_" + name, align_bytes=64) for name in "iec"}
+
+        def gather_scales(name):
+            nc.vector.tensor_copy(picked_sc[name][:], tab_sc[:].bitcast(U8).indirect(lists[name][:]))
+
+        def move_plane(name):
+            nc.sync.dma_start(second_plane[name][0 : P - PASS_GAP, :], picked_sc[name][PASS_GAP:P, :].bitcast(I32))
+
         nc.sync.dma_start(lists["i"][:], offs3)
         nc.sync.dma_start(wi_w[:], wi8_words.rearrange("a p y i -> p a (y i)").bitcast(I32))
         nc.sync.dma_start(lists["c"][:], offs2)
         tab_sc_hbm = tab_scales.bitcast(I32)
         for r in range(4):
             nc.sync.dma_start(tab_sc[r:P:PASS_GAP, :], tab_sc_hbm[:, r:16:4, :].rearrange("a q n -> q a n"))
-        load_tab(0)
+        load_tab(0, 0)
         load_planes(wi_sc, wi8_scales, nc.sync)
+        load_tab(0, 1)
         nc.sync.dma_start(ws_w[:], ws4_words.rearrange("a p y -> p a y").bitcast(I32))
-        load_tab(1)
-        nc.sync.dma_start(lists["e"][:], offs)
         load_planes(ws_sc, ws4_scales, nc.sync)
-        for part in range(4):
+        load_tab(1, 0)
+        load_tab(1, 1)
+        for name in "ic":
+            gather_scales(name)
+            move_plane(name)
+        load_we(0)
+        nc.sync.dma_start(lists["e"][:], offs)
+        for part in range(1, 4):
             load_we(part)
         nc.sync.dma_start(st_w[:], st4_words[0].bitcast(I32))
         with nc.allow_non_contiguous_dma(reason="one bias value a partition"):
@@ -109,18 +126,15 @@ def tile_list_inhibited_enzyme_fluxes_kernel(
         def deal_plane(into, plane):
             nc.gpsimd.tensor_copy(into[:], plane[:].rearrange("p a y -> p (a y)").bitcast(U8).rearrange("p (m t) -> p t m", t=SLOTS))
 
-        picked_sc = {name: keep.tile([P, S], U8, name="picked_sc_" + name, align_bytes=64) for name in "iec"}
         picked_w = {}
 
-        def gather_scales(name, queue):
-            nc.vector.tensor_copy(picked_sc[name][:], tab_sc[:].bitcast(U8).indirect(lists[name][:]))
-            queue.dma_start(second_plane[name][0 : P - PASS_GAP, :], picked_sc[name][PASS_GAP:P, :].bitcast(I32))
 
-        def gather_words(name, a, ch, into=None):
-            cols = slice(ch * CHUNK // 16, (ch + 1) * CHUNK // 16)
+        def gather_words(name, a, chunks, into=None):
+            cols = slice(chunks[0] * CHUNK // 16, (chunks[-1] + 1) * CHUNK // 16)
             if into is None:
-                into = keep.tile([P, CHUNK], U32, name="picked_w_%s%d%d" % (name, a, ch), align_bytes=64)[:]
-            picked_w[name, a, ch] = into
+                into = keep.tile([P, len(chunks) * CHUNK], U32, name="picked_w_%s%d%d" % (name, a, chunks[0]), align_bytes=64)[:]
+            for place, ch in enumerate(chunks):
+                picked_w[name, a, ch] = into[:, place * CHUNK : (place + 1) * CHUNK]
             nc.vector.tensor_copy(into, tab_w[a][:].bitcast(U32).indirect(lists[name][:, cols]))
 
         we_bf = reused.tile([P, PASSES, SLOTS, BLOCK, SLOTS], BF16, offset=ROUNDED_WE_AT, align_bytes=64)
@@ -187,13 +201,10 @@ def tile_list_inhibited_enzyme_fluxes_kernel(
         def inverse_root(first):
             nc.scalar.activation(roots[first // 2][:], squares[first // 2][:], ACT.Abs_reciprocal_sqrt, bias=1.0)
 
-        def damping(first, on_gpsimd=False):
+        def damping(first):
             root = roots[first // 2][:]
             into = keep.tile([P, 2, H], F32, name="damp%d" % first)
-            if on_gpsimd:
-                nc.gpsimd.tensor_tensor(into[:], root, root, MULT)
-            else:
-                nc.scalar.activation(into[:], root, ACT.Square)
+            nc.scalar.activation(into[:], root, ACT.Square)
             for g in range(2):
                 damp[first + g] = into[:, g, :]
 
@@ -254,29 +265,23 @@ def tile_list_inhibited_enzyme_fluxes_kernel(
 
         nc.gpsimd.tensor_copy(wi_dealt[:].rearrange("p t (g i) -> p g t i", i=4),
                               wi_w[:].rearrange("p a (g i t) -> p (a g) t i", i=4, t=SLOTS))
-        gather_scales("i", nc.gpsimd)
-        gather_scales("c", nc.gpsimd)
         deal_plane(wi_sc_dealt, wi_sc)
         nc.gpsimd.tensor_copy(ws_dealt[:], ws_w[:].rearrange("p a y -> p (a y)").bitcast(U8).rearrange("p (m t h) -> p t m h", t=SLOTS, h=2))
         deal_plane(ws_sc_dealt, ws_sc)
-        for a in range(PASSES):
-            for ch in range(CHUNKS):
-                for name in "ic":
-                    gather_words(name, a, ch)
-            for blk in range(4):
-                multiply_pass("i", blk, blk, a)
-        gather_scales("e", nc.sync)
-        for a in range(PASSES):
-            gather_words("e", a, 0)
+        gather_words("i", 0, (0, 1))
+        gather_words("c", 0, (0, 1))
+        for blk in range(4):
+            multiply_pass("i", blk, blk, 0)
+        gather_words("i", 1, (0,))
+        for blk in range(4):
+            multiply_pass("i", blk, blk, 1)
+        gather_words("c", 1, (0, 1))
+        gather_words("i", 1, (1,))
+        gather_scales("e")
+        move_plane("e")
+        gather_words("e", 0, (0, 1))
         for part in range(4):
             round_we(part)
-        nc.vector.quantize_mx(out=we_w[:].rearrange("p a t m -> p (a t m)").bitcast(FP8X4),
-                              scales=we_sc[:].rearrange("p a t m -> p (a t m)"),
-                              in_=we_bf[:].rearrange("p a t m j -> p (a t m j)"))
-        late_words = reused.tile([P, PASSES, CHUNK], U32, offset=LATE_WORDS_AT, align_bytes=64)
-        for a in range(PASSES):
-            gather_words("e", a, 1, late_words[:, a, :])
-
         for blk in range(4):
             multiply("c", blk, 4 + blk)
         square_inhibitor(0)
@@ -285,11 +290,19 @@ def tile_list_inhibited_enzyme_fluxes_kernel(
         square_inhibitor(2)
         square_inhibitor(3)
         inverse_root(2)
-        damping(2, on_gpsimd=True)
+        nc.vector.quantize_mx(out=we_w[:].rearrange("p a t m -> p (a t m)").bitcast(FP8X4),
+                              scales=we_sc[:].rearrange("p a t m -> p (a t m)"),
+                              in_=we_bf[:].rearrange("p a t m j -> p (a t m j)"))
+        late_words = reused.tile([P, PASSES, CHUNK], U32, offset=LATE_WORDS_AT, align_bytes=64)
+        for ch in range(CHUNKS):
+            gather_words("e", 1, (ch,), late_words[:, ch, :])
+
         damping(0)
         for blk in range(4):
+            if blk == 2:
+                damping(2)
             copy_substrate(blk, LAST_LEVEL_AT if blk == 3 else None)
-            damp_substrate(blk, LATE_DAMPED_AT if blk == 0 else None)
+            damp_substrate(blk, LATE_DAMPED_AT[blk])
             multiply("i", 4 + blk, 4 + blk)
         for blk in range(4, BLOCKS):
             multiply("c", blk, blk - 4)

@@ -27,11 +27,12 @@ BLOCKS = S // BLOCK
 PASS_GAP = 16
 
 ROUNDED_WE_AT = 4096
-SECOND_PASS_AT = 32768
-LATE_PAIRS_AT = {4: SECOND_PASS_AT, 6: SECOND_PASS_AT + 4096}
-LATE_WORDS_AT = ROUNDED_WE_AT + 64 - 4096
-LATE_DAMPED_AT = [ROUNDED_WE_AT + 64, ROUNDED_WE_AT + 64 + 2048, ROUNDED_WE_AT + 64 + 4096, ROUNDED_WE_AT + 8192 - 64]
-LAST_LEVEL_AT = 20480
+RATES_AT = {(0, 1): 24576, (2, 3): 26624}
+H_WORDS_AT = {(0, 1): 28672, (2, 3): 30720}
+LATE_WORDS_AT = ROUNDED_WE_AT
+DAMPED_AT = {2: ROUNDED_WE_AT + 2048, 3: ROUNDED_WE_AT + 4096, 4: RATES_AT[0, 1], 5: RATES_AT[2, 3], 6: RATES_AT[0, 1], 7: RATES_AT[2, 3]}
+WE_WORDS_AT = 16384
+LEVELS_AT = {0: WE_WORDS_AT, 1: WE_WORDS_AT + 2048, 3: H_WORDS_AT[0, 1], 4: H_WORDS_AT[2, 3]}
 
 
 def tile_list_inhibited_enzyme_fluxes_kernel(
@@ -46,8 +47,7 @@ def tile_list_inhibited_enzyme_fluxes_kernel(
 
         lists = {name: keep.tile([P, S // 16], U16, name="list_" + name) for name in "iec"}
         tab_sc = keep.tile([P, T // 4], I32, align_bytes=64)
-        tab_w = [keep.tile([P, T], I32, name="tab_w0", align_bytes=64),
-                 reused.tile([P, T], I32, name="tab_w1", offset=SECOND_PASS_AT, align_bytes=64)]
+        tab_w = [keep.tile([P, T], I32, name="tab_w%d" % a, align_bytes=64) for a in range(PASSES)]
         wi_w = keep.tile([P, PASSES, H], I32, align_bytes=64)
         ws_w = keep.tile([P, PASSES, H // 2], I32, align_bytes=64)
         st_w = keep.tile([P, N // 2], I32, align_bytes=64)
@@ -138,7 +138,7 @@ def tile_list_inhibited_enzyme_fluxes_kernel(
             nc.vector.tensor_copy(into, tab_w[a][:].bitcast(U32).indirect(lists[name][:, cols]))
 
         we_bf = reused.tile([P, PASSES, SLOTS, BLOCK, SLOTS], BF16, offset=ROUNDED_WE_AT, align_bytes=64)
-        we_w = keep.tile([P, PASSES, SLOTS, BLOCK], U32, align_bytes=64)
+        we_w = reused.tile([P, PASSES, SLOTS, BLOCK], U32, offset=WE_WORDS_AT, align_bytes=64)
         we_sc = keep.tile([P, PASSES, SLOTS, BLOCK], U8, align_bytes=64)
 
         def round_we(part):
@@ -189,7 +189,9 @@ def tile_list_inhibited_enzyme_fluxes_kernel(
 
         squares = [keep.tile([P, 2, H], F32, name="squares%d" % pair) for pair in range(BLOCKS // 2)]
         roots = [keep.tile([P, 2, H], F32, name="roots%d" % pair) for pair in range(BLOCKS // 2)]
-        rates = [keep.tile([P, 2, H], BF16, name="rates%d" % pair, align_bytes=64) for pair in range(BLOCKS // 2)]
+        rates = {group: reused.tile([P, 2, H], BF16, name="rates%d" % group[0], offset=at, align_bytes=64)[:] for group, at in RATES_AT.items()}
+        last_rates = [keep.tile([P, 2, H], BF16, name="last_rates%d" % pair, align_bytes=64) for pair in range(2)]
+        rates = dict(list(rates.items()) + list({(4, 5): last_rates[0][:], (6,): last_rates[1][:, 0:1, :], (7,): last_rates[1][:, 1:2, :]}.items()))
         damp = {}
         levels = {}
         damped = {}
@@ -208,49 +210,41 @@ def tile_list_inhibited_enzyme_fluxes_kernel(
             for g in range(2):
                 damp[first + g] = into[:, g, :]
 
-        def copy_substrate(blk, at=None):
+        def placed(name, shape, dtype, at):
             if at is None:
-                levels[blk] = keep.tile([P, H], F32, name="level%d" % blk)
-            else:
-                levels[blk] = reused.tile([P, H], F32, name="level%d" % blk, offset=at, align_bytes=64)
+                return keep.tile([P] + shape, dtype, name=name, align_bytes=64)
+            return reused.tile([P] + shape, dtype, name=name, offset=at, align_bytes=64)
+
+        def copy_substrate(blk):
+            levels[blk] = placed("level%d" % blk, [H], F32, LEVELS_AT.get(blk))
             nc.scalar.copy(woven(levels[blk][:]), sums["c", blk])
 
-        def damp_substrate(blk, at=None):
-            if blk in LATE_PAIRS_AT:
-                pair = reused.tile([P, 2, H], F32, name="damped%d" % blk, offset=LATE_PAIRS_AT[blk], align_bytes=64)
-                damped[blk], damped[blk + 1] = pair[:, 0, :], pair[:, 1, :]
-            elif at is not None:
-                damped[blk] = reused.tile([P, H], F32, name="damped%d" % blk, offset=at, align_bytes=64)[:]
-            elif blk not in damped:
-                damped[blk] = keep.tile([P, H], F32, name="damped%d" % blk)[:]
+        def damp_substrate(blk):
+            damped[blk] = placed("damped%d" % blk, [H], F32, DAMPED_AT.get(blk))[:]
             if blk in levels:
                 nc.gpsimd.tensor_tensor(damped[blk], levels[blk][:], damp[blk], MULT)
             else:
                 nc.vector.tensor_tensor(woven(damped[blk]), woven(damp[blk]), sums["c", blk], MULT)
 
         def rate(blk):
-            nc.vector.tensor_tensor(woven(rates[blk // 2][:, blk % 2, :]), woven(damped[blk]), sums["e", blk], MULT)
+            group = [g for g in rates if blk in g][0]
+            nc.vector.tensor_tensor(woven(rates[group][:, blk - group[0], :]), woven(damped[blk]), sums["e", blk], MULT)
 
-        def quantise_rates(group, at=None):
+        def quantise_rates(group):
             width = len(group) * BLOCK
-            if at is None:
-                h_w = keep.tile([P, width], U32, name="h_w%d" % group[0], align_bytes=64)
-            else:
-                h_w = reused.tile([P, width], U32, name="h_w%d" % group[0], offset=at, align_bytes=64)
+            h_w = placed("h_w%d" % group[0], [width], U32, H_WORDS_AT.get(group))
             h_sc = keep.tile([P, width], U8, name="h_sc%d" % group[0], align_bytes=64)
-            first = group[0] % 2
-            nc.vector.quantize_mx(out=h_w[:].bitcast(FP8X4), scales=h_sc[:],
-                                  in_=rates[group[0] // 2][:, first : first + len(group), :].rearrange("p g x -> p (g x)"))
+            nc.vector.quantize_mx(out=h_w[:].bitcast(FP8X4), scales=h_sc[:], in_=rates[group].rearrange("p g x -> p (g x)"))
             h_mx[group] = h_w, h_sc
 
-        def flux(group, first, bank, on_vector=False):
+        def flux(group, first, bank, on_vector=False, count=2):
             h_w, h_sc = h_mx[group]
             width = len(group) * BLOCK
             st_bytes = st_w[:].bitcast(U8)
             st_plane = st_sc[:].bitcast(U8)
-            result = keep.tile([P, 2, width], F32, name="result%d_%d" % (group[0], first))
-            y = take_bank(bank, [2, width])
-            for c in range(first, first + 2):
+            result = keep.tile([P, count, width], F32, name="result%d_%d" % (group[0], first))
+            y = take_bank(bank, [count, width])
+            for c in range(first, first + count):
                 nc.tensor.matmul_mx(out=y[:, c - first, :], lhsT=st_bytes[:, 2 * P * c : 2 * P * (c + 1)].bitcast(FP4X4),
                                     lhsT_scale=st_plane[:, P * c : P * (c + 1)],
                                     rhs=h_w[:].bitcast(FP8X4), rhs_scale=h_sc[:], start=True, stop=True)
@@ -258,9 +252,9 @@ def tile_list_inhibited_enzyme_fluxes_kernel(
                 spread = bias[:, first : first + 2].unsqueeze(2).to_broadcast([P, 2, width])
                 nc.vector.tensor_tensor(result[:], spread, y[:], ADD)
             else:
-                for c in range(first, first + 2):
+                for c in range(first, first + count):
                     nc.scalar.activation(result[:, c - first, :], y[:, c - first, :], ACT.Identity, bias=bias[:, c : c + 1])
-            rows = out[first * P : (first + 2) * P, group[0] * BLOCK : group[0] * BLOCK + width]
+            rows = out[first * P : (first + count) * P, group[0] * BLOCK : group[0] * BLOCK + width]
             nc.sync.dma_start(rows.rearrange("(c p) j -> p c j", p=P), result[:])
 
         nc.gpsimd.tensor_copy(wi_dealt[:].rearrange("p t (g i) -> p g t i", i=4),
@@ -280,64 +274,69 @@ def tile_list_inhibited_enzyme_fluxes_kernel(
         gather_scales("e")
         move_plane("e")
         gather_words("e", 0, (0, 1))
+        gather_words("e", 1, (0,))
         for part in range(4):
             round_we(part)
         for blk in range(4):
             multiply("c", blk, 4 + blk)
         square_inhibitor(0)
         square_inhibitor(1)
-        inverse_root(0)
         square_inhibitor(2)
+        inverse_root(0)
         square_inhibitor(3)
+        damping(0)
+        copy_substrate(0)
         inverse_root(2)
+        copy_substrate(1)
+        damp_substrate(0)
+        damp_substrate(1)
         nc.vector.quantize_mx(out=we_w[:].rearrange("p a t m -> p (a t m)").bitcast(FP8X4),
                               scales=we_sc[:].rearrange("p a t m -> p (a t m)"),
                               in_=we_bf[:].rearrange("p a t m j -> p (a t m j)"))
-        late_words = reused.tile([P, PASSES, CHUNK], U32, offset=LATE_WORDS_AT, align_bytes=64)
-        for ch in range(CHUNKS):
-            gather_words("e", 1, (ch,), late_words[:, ch, :])
+        late_words = reused.tile([P, CHUNK], U32, offset=LATE_WORDS_AT, align_bytes=64)
+        gather_words("e", 1, (1,), late_words[:])
 
-        damping(0)
-        for blk in range(4):
-            if blk == 2:
-                damping(2)
-            copy_substrate(blk, LAST_LEVEL_AT if blk == 3 else None)
-            damp_substrate(blk, LATE_DAMPED_AT[blk])
-            multiply("i", 4 + blk, 4 + blk)
+        multiply("i", 4, 4)
+        multiply("i", 5, 5)
         for blk in range(4, BLOCKS):
             multiply("c", blk, blk - 4)
-        for first in (4, 6):
-            for blk in (first, first + 1):
-                square_inhibitor(blk)
-                multiply("e", blk - 4, blk)
-            inverse_root(first)
-            damping(first)
+        damping(2)
+        for blk in (2, 3):
+            copy_substrate(blk)
+            damp_substrate(blk)
+            multiply("i", 4 + blk, 4 + blk)
+        for blk in (4, 5, 6):
+            square_inhibitor(blk)
+            multiply("e", blk - 4, blk)
+        inverse_root(4)
+        square_inhibitor(7)
+        multiply("e", 3, 7)
+        damping(4)
+        copy_substrate(4)
+        inverse_root(6)
+        copy_substrate(5)
+        damping(6)
 
-        for blk in range(2):
-            rate(blk)
-            multiply("e", 4 + blk, 4 + blk)
-        damp_substrate(4)
-        damp_substrate(5)
-        quantise_rates((0, 1), LAST_LEVEL_AT)
+        for first in (0, 2):
+            for blk in (first, first + 1):
+                rate(blk)
+                multiply("e", 4 + blk, 4 + blk)
+            quantise_rates((first, first + 1))
+            damp_substrate(4 + first // 2)
         flux((0, 1), 0, 0)
         flux((0, 1), 2, 1)
         rate(4)
+        flux((2, 3), 0, 4)
         rate(5)
-        rate(2)
-        multiply("e", 6, 6)
-        quantise_rates((4, 5))
-        flux((4, 5), 0, 4)
-        flux((4, 5), 2, 5)
-        rate(3)
-        multiply("e", 7, 7)
+        flux((2, 3), 2, 5)
         damp_substrate(6)
-        quantise_rates((2, 3))
-        flux((2, 3), 0, 0)
-        flux((2, 3), 2, 1)
+        quantise_rates((4, 5))
+        flux((4, 5), 0, 0)
+        flux((4, 5), 2, 1)
         damp_substrate(7)
         rate(6)
         rate(7)
-        for group, banks in (((6,), (2, 3)), ((7,), (4, 5))):
+        for group, banks in (((6,), (2, 3)), ((7,), (6, 7))):
             quantise_rates(group)
             flux(group, 0, banks[0])
             flux(group, 2, banks[1], on_vector=True)

@@ -200,14 +200,14 @@ def tile_list_inhibited_enzyme_fluxes_kernel(
         def square_inhibitor(blk):
             nc.scalar.activation(woven(squares[blk // 2][:, blk % 2, :]), sums["i", blk], ACT.Square)
 
-        def inverse_root(first):
-            nc.scalar.activation(roots[first // 2][:], squares[first // 2][:], ACT.Abs_reciprocal_sqrt, bias=1.0)
+        def inverse_root(first, count=2):
+            part = slice(first % 2, first % 2 + count)
+            nc.scalar.activation(roots[first // 2][:, part, :], squares[first // 2][:, part, :], ACT.Abs_reciprocal_sqrt, bias=1.0)
 
-        def damping(first):
-            root = roots[first // 2][:]
-            into = keep.tile([P, 2, H], F32, name="damp%d" % first)
-            nc.scalar.activation(into[:], root, ACT.Square)
-            for g in range(2):
+        def damping(first, count=2):
+            into = keep.tile([P, count, H], F32, name="damp%d" % first)
+            nc.scalar.activation(into[:], roots[first // 2][:, first % 2 : first % 2 + count, :], ACT.Square)
+            for g in range(count):
                 damp[first + g] = into[:, g, :]
 
         def placed(name, shape, dtype, at):
@@ -309,34 +309,43 @@ def tile_list_inhibited_enzyme_fluxes_kernel(
             square_inhibitor(blk)
             multiply("e", blk - 4, blk)
         inverse_root(4)
-        square_inhibitor(7)
-        multiply("e", 3, 7)
-        damping(4)
         copy_substrate(4)
-        inverse_root(6)
+        multiply("e", 3, 0)
+        damping(4)
+        square_inhibitor(7)
         copy_substrate(5)
-        damping(6)
+        for step in (inverse_root, damping):
+            for blk in (6, 7):
+                step(blk, count=1)
 
-        for first in (0, 2):
-            for blk in (first, first + 1):
-                rate(blk)
-                multiply("e", 4 + blk, 4 + blk)
-            quantise_rates((first, first + 1))
-            damp_substrate(4 + first // 2)
-        flux((0, 1), 0, 0)
-        flux((0, 1), 2, 1)
+        rate(0)
+        multiply("e", 4, 4)
+        rate(1)
+        quantise_rates((0, 1))
+        damp_substrate(4)
+        rate(2)
+        rate(3)
+        flux((0, 1), 0, 5, on_vector=True)
+        flux((0, 1), 2, 6)
+        multiply("e", 5, 7)
+        multiply("e", 6, 1)
+        multiply("e", 7, 0)
+        quantise_rates((2, 3))
+        damp_substrate(5)
         rate(4)
-        flux((2, 3), 0, 4)
-        rate(5)
-        flux((2, 3), 2, 5)
+        flux((2, 3), 0, 5)
+        flux((2, 3), 2, 4)
         damp_substrate(6)
-        quantise_rates((4, 5))
-        flux((4, 5), 0, 0)
-        flux((4, 5), 2, 1)
-        damp_substrate(7)
+        rate(5)
         rate(6)
+        quantise_rates((4, 5))
+        flux((4, 5), 0, 6)
+        flux((4, 5), 2, 7)
+        damp_substrate(7)
+        quantise_rates((6,))
+        flux((6,), 0, 2)
+        flux((6,), 2, 1)
         rate(7)
-        for group, banks in (((6,), (2, 3)), ((7,), (6, 7))):
-            quantise_rates(group)
-            flux(group, 0, banks[0])
-            flux(group, 2, banks[1], on_vector=True)
+        quantise_rates((7,))
+        flux((7,), 0, 3)
+        flux((7,), 2, 0, on_vector=True)

@@ -27,12 +27,12 @@ BLOCKS = S // BLOCK
 PASS_GAP = 16
 
 ROUNDED_WE_AT = 4096
-RATES_AT = {(0, 1): 24576, (2, 3): 26624}
-H_WORDS_AT = {(0, 1): 28672, (2, 3): 30720}
+RATES_AT = {(0, 1): 24576, (2, 3): 26624, (4, 5): 28672}
 LATE_WORDS_AT = ROUNDED_WE_AT
-DAMPED_AT = {2: ROUNDED_WE_AT + 2048, 3: ROUNDED_WE_AT + 4096, 4: RATES_AT[0, 1], 5: RATES_AT[2, 3], 6: RATES_AT[0, 1], 7: RATES_AT[2, 3]}
+DAMPED_AT = {2: ROUNDED_WE_AT + 2048, 3: ROUNDED_WE_AT + 4096, 4: ROUNDED_WE_AT + 6144,
+             5: RATES_AT[0, 1], 6: RATES_AT[2, 3], 7: RATES_AT[4, 5]}
 WE_WORDS_AT = 16384
-LEVELS_AT = {0: WE_WORDS_AT, 1: WE_WORDS_AT + 2048, 3: H_WORDS_AT[0, 1], 4: H_WORDS_AT[2, 3]}
+LEVELS_AT = {0: WE_WORDS_AT, 1: WE_WORDS_AT + 2048}
 
 
 def tile_list_inhibited_enzyme_fluxes_kernel(
@@ -190,8 +190,8 @@ def tile_list_inhibited_enzyme_fluxes_kernel(
         squares = [keep.tile([P, 2, H], F32, name="squares%d" % pair) for pair in range(BLOCKS // 2)]
         roots = [keep.tile([P, 2, H], F32, name="roots%d" % pair) for pair in range(BLOCKS // 2)]
         rates = {group: reused.tile([P, 2, H], BF16, name="rates%d" % group[0], offset=at, align_bytes=64)[:] for group, at in RATES_AT.items()}
-        last_rates = [keep.tile([P, 2, H], BF16, name="last_rates%d" % pair, align_bytes=64) for pair in range(2)]
-        rates = dict(list(rates.items()) + list({(4, 5): last_rates[0][:], (6,): last_rates[1][:, 0:1, :], (7,): last_rates[1][:, 1:2, :]}.items()))
+        for blk in (6, 7):
+            rates[(blk,)] = keep.tile([P, 1, H], BF16, name="rates%d" % blk, align_bytes=64)[:]
         damp = {}
         levels = {}
         damped = {}
@@ -232,7 +232,7 @@ def tile_list_inhibited_enzyme_fluxes_kernel(
 
         def quantise_rates(group):
             width = len(group) * BLOCK
-            h_w = placed("h_w%d" % group[0], [width], U32, H_WORDS_AT.get(group))
+            h_w = keep.tile([P, width], U32, name="h_w%d" % group[0], align_bytes=64)
             h_sc = keep.tile([P, width], U8, name="h_sc%d" % group[0], align_bytes=64)
             nc.vector.quantize_mx(out=h_w[:].bitcast(FP8X4), scales=h_sc[:], in_=rates[group].rearrange("p g x -> p (g x)"))
             h_mx[group] = h_w, h_sc
@@ -301,46 +301,46 @@ def tile_list_inhibited_enzyme_fluxes_kernel(
         for blk in range(4, BLOCKS):
             multiply("c", blk, blk - 4)
         damping(2)
-        for blk in (2, 3):
-            copy_substrate(blk)
-            damp_substrate(blk)
-            multiply("i", 4 + blk, 4 + blk)
+        copy_substrate(2)
+        multiply("i", 6, 6)
+        damp_substrate(2)
+        damp_substrate(3)
         for blk in (4, 5, 6):
             square_inhibitor(blk)
             multiply("e", blk - 4, blk)
+        multiply("i", 7, 7)
         inverse_root(4)
-        copy_substrate(4)
-        multiply("e", 3, 0)
+        inverse_root(6, count=1)
         damping(4)
         square_inhibitor(7)
-        copy_substrate(5)
-        for step in (inverse_root, damping):
-            for blk in (6, 7):
-                step(blk, count=1)
+        damping(6, count=1)
+        inverse_root(7, count=1)
 
-        rate(0)
-        multiply("e", 4, 4)
-        rate(1)
-        quantise_rates((0, 1))
         damp_substrate(4)
+        rate(0)
+        multiply("e", 3, 4)
+        rate(1)
+        multiply("e", 4, 5)
         rate(2)
+        quantise_rates((0, 1))
+        flux((0, 1), 0, 6)
+        damping(7, count=1)
+        multiply("e", 5, 0)
         rate(3)
-        flux((0, 1), 0, 5, on_vector=True)
-        flux((0, 1), 2, 6)
-        multiply("e", 5, 7)
-        multiply("e", 6, 1)
-        multiply("e", 7, 0)
-        quantise_rates((2, 3))
+        flux((0, 1), 2, 4)
+        multiply("e", 7, 7)
         damp_substrate(5)
-        rate(4)
-        flux((2, 3), 0, 5)
+        multiply("e", 6, 1)
+        quantise_rates((2, 3))
+        flux((2, 3), 0, 6)
         flux((2, 3), 2, 4)
+        rate(4)
         damp_substrate(6)
         rate(5)
         rate(6)
         quantise_rates((4, 5))
-        flux((4, 5), 0, 6)
-        flux((4, 5), 2, 7)
+        flux((4, 5), 0, 5)
+        flux((4, 5), 2, 0)
         damp_substrate(7)
         quantise_rates((6,))
         flux((6,), 0, 2)
@@ -348,4 +348,4 @@ def tile_list_inhibited_enzyme_fluxes_kernel(
         rate(7)
         quantise_rates((7,))
         flux((7,), 0, 3)
-        flux((7,), 2, 0, on_vector=True)
+        flux((7,), 2, 7, on_vector=True)

from contextlib import ExitStack

import concourse.mybir as mybir

K, T, S, H, N = 1024, 4096, 1024, 512, 512
FLOPS = 2 * S * (3 * K * H + H * N)

F32 = mybir.dt.float32
BF16 = mybir.dt.bfloat16
I32 = mybir.dt.int32
U32 = mybir.dt.uint32
U16 = mybir.dt.uint16
U8 = mybir.dt.uint8
FP8X4 = mybir.dt.float8_e4m3fn_x4
FP4X4 = mybir.dt.float4_e2m1fn_x4
ACT = mybir.ActivationFunctionType
MULT = mybir.AluOpType.mult
ADD = mybir.AluOpType.add

P = 128
PASSES = K // 512
SLOTS = 4
CHUNK = 512
BLOCK = 128
CHUNKS = S // CHUNK
BLOCKS = S // BLOCK
PASS_GAP = 16

ROUNDED_WE_AT = 4096
RATES_AT = {(0, 1): 24576, (2, 3): 26624, (4, 5): 28672}
LATE_WORDS_AT = ROUNDED_WE_AT
DAMPED_AT = {2: ROUNDED_WE_AT + 2048, 3: ROUNDED_WE_AT + 4096, 4: ROUNDED_WE_AT + 6144,
             5: RATES_AT[0, 1], 6: RATES_AT[2, 3], 7: RATES_AT[4, 5]}
WE_WORDS_AT = 16384
LEVELS_AT = {0: WE_WORDS_AT, 1: WE_WORDS_AT + 2048}


def tile_list_inhibited_enzyme_fluxes_kernel(
    tc, tab_words, tab_scales, offs, offs2, offs3, we, ws4_words, ws4_scales,
    wi8_words, wi8_scales, st4_words, st4_scales, b, out,
):
    nc = tc.nc
    with ExitStack() as ctx:
        keep = ctx.enter_context(tc.tile_pool(name="keep", bufs=1))
        reused = ctx.enter_context(tc.tile_pool(name="reused", bufs=1))
        psum = ctx.enter_context(tc.psum_pool(name="psum", bufs=1))

        lists = {name: keep.tile([P, S // 16], U16, name="list_" + name) for name in "iec"}
        tab_sc = keep.tile([P, T // 4], I32, align_bytes=64)
        tab_w = [keep.tile([P, T], I32, name="tab_w%d" % a, align_bytes=64) for a in range(PASSES)]
        wi_w = keep.tile([P, PASSES, H], I32, align_bytes=64)
        ws_w = keep.tile([P, PASSES, H // 2], I32, align_bytes=64)
        st_w = keep.tile([P, N // 2], I32, align_bytes=64)
        wi_sc = keep.tile([P, PASSES, H // 4], I32, align_bytes=64)
        ws_sc = keep.tile([P, PASSES, H // 4], I32, align_bytes=64)
        st_sc = keep.tile([P, N // 4], I32, align_bytes=64)
        we_raw = [keep.tile([P, SLOTS, H // 2], F32, name="we_raw%d" % part) for part in range(4)]
        bias = keep.tile([P, N // P], F32)
        second_plane = {name: keep.tile([P, S // 4], I32, name="second_plane_" + name, align_bytes=64) for name in "iec"}
        warm_in = keep.tile([P, 1], F32)
        warm_out = keep.tile([P, 1], F32)

        nc.vector.memset(tab_sc[:], 0)
        nc.vector.memset(warm_in[:], 1.0)
        nc.scalar.activation(warm_out[:], warm_in[:], ACT.Abs_reciprocal_sqrt)
        nc.vector.memset(wi_sc[:], 0)
        nc.vector.memset(ws_sc[:], 0)
        nc.vector.memset(st_sc[:], 0)
        for name in "iec":
            nc.vector.memset(second_plane[name][:], 0)

        def load_tab(a, half):
            cols = slice(half * T // 2, (half + 1) * T // 2)
            nc.sync.dma_start(tab_w[a][:, cols], tab_words[a].rearrange("p t i -> p (t i)").bitcast(I32)[:, cols])

        def load_planes(tile, scales, queue):
            hbm = scales.bitcast(I32)
            for r in range(4):
                queue.dma_start(tile[r:P:32, :, :], hbm[:, r:16:4, :].rearrange("a q n -> q a n"))

        def load_we(part):
            a, half = divmod(part, 2)
            rows = we[512 * a : 512 * (a + 1), half * H // 2 : (half + 1) * H // 2]
            nc.sync.dma_start(we_raw[part][:], rows.rearrange("(p j) r -> p j r", j=SLOTS))

        picked_sc = {name: keep.tile([P, S], U8, name="picked_sc_" + name, align_bytes=64) for name in "iec"}

        def gather_scales(name):
            nc.vector.tensor_copy(picked_sc[name][:], tab_sc[:].bitcast(U8).indirect(lists[name][:]))

        def move_plane(name):
            nc.sync.dma_start(second_plane[name][0 : P - PASS_GAP, :], picked_sc[name][PASS_GAP:P, :].bitcast(I32))

        nc.sync.dma_start(lists["i"][:], offs3)
        nc.sync.dma_start(wi_w[:], wi8_words.rearrange("a p y i -> p a (y i)").bitcast(I32))
        nc.sync.dma_start(lists["c"][:], offs2)
        tab_sc_hbm = tab_scales.bitcast(I32)
        for r in range(4):
            nc.sync.dma_start(tab_sc[r:P:PASS_GAP, :], tab_sc_hbm[:, r:16:4, :].rearrange("a q n -> q a n"))
        load_tab(0, 0)
        load_planes(wi_sc, wi8_scales, nc.sync)
        load_tab(0, 1)
        nc.sync.dma_start(ws_w[:], ws4_words.rearrange("a p y -> p a y").bitcast(I32))
        load_planes(ws_sc, ws4_scales, nc.sync)
        load_tab(1, 0)
        load_tab(1, 1)
        for name in "ic":
            gather_scales(name)
            move_plane(name)
        load_we(0)
        nc.sync.dma_start(lists["e"][:], offs)
        for part in range(1, 4):
            load_we(part)
        nc.sync.dma_start(st_w[:], st4_words[0].bitcast(I32))
        with nc.allow_non_contiguous_dma(reason="one bias value a partition"):
            nc.sync.dma_start(bias[:], b.rearrange("(c p) -> p c", p=P))
        st_sc_hbm = st4_scales.bitcast(I32)
        for r in range(4):
            nc.sync.dma_start(st_sc[r:P:32, :], st_sc_hbm[0, r:16:4, :])

        wi_dealt = keep.tile([P, SLOTS, PASSES * BLOCK], I32, align_bytes=64)
        ws_dealt = keep.tile([P, SLOTS, PASSES * BLOCK, 2], U8, align_bytes=64)
        wi_sc_dealt = keep.tile([P, SLOTS, PASSES * BLOCK], U8, align_bytes=64)
        ws_sc_dealt = keep.tile([P, SLOTS, PASSES * BLOCK], U8, align_bytes=64)

        def deal_plane(into, plane):
            nc.gpsimd.tensor_copy(into[:], plane[:].rearrange("p a y -> p (a y)").bitcast(U8).rearrange("p (m t) -> p t m", t=SLOTS))

        picked_w = {}


        def gather_words(name, a, chunks, into=None):
            cols = slice(chunks[0] * CHUNK // 16, (chunks[-1] + 1) * CHUNK // 16)
            if into is None:
                into = keep.tile([P, len(chunks) * CHUNK], U32, name="picked_w_%s%d%d" % (name, a, chunks[0]), align_bytes=64)[:]
            for place, ch in enumerate(chunks):
                picked_w[name, a, ch] = into[:, place * CHUNK : (place + 1) * CHUNK]
            nc.vector.tensor_copy(into, tab_w[a][:].bitcast(U32).indirect(lists[name][:, cols]))

        we_bf = reused.tile([P, PASSES, SLOTS, BLOCK, SLOTS], BF16, offset=ROUNDED_WE_AT, align_bytes=64)
        we_w = reused.tile([P, PASSES, SLOTS, BLOCK], U32, offset=WE_WORDS_AT, align_bytes=64)
        we_sc = keep.tile([P, PASSES, SLOTS, BLOCK], U8, align_bytes=64)

        def round_we(part):
            a, half = divmod(part, 2)
            into = we_bf[:, a, :, half * BLOCK // 2 : (half + 1) * BLOCK // 2, :]
            nc.gpsimd.tensor_scalar(into.rearrange("p t m j -> p m t j"),
                                    we_raw[part][:].rearrange("p j (m t) -> p m t j", t=SLOTS), 1.0, 0.0, MULT, ADD)

        def take_bank(bank, shape):
            return psum.tile([P] + shape, F32, name="bank%d" % bank, tag="bank%d" % bank)

        def stationary(name, a, t):
            cols = slice(a * BLOCK, (a + 1) * BLOCK)
            if name == "i":
                return wi_dealt[:, t, cols].bitcast(FP8X4), wi_sc_dealt[:, t, cols]
            if name == "e":
                return we_w[:, a, t, :].bitcast(FP8X4), we_sc[:, a, t, :]
            return ws_dealt[:, t, cols, :].rearrange("p m h -> p (m h)").bitcast(FP4X4), ws_sc_dealt[:, t, cols]

        accumulators = {}
        sums = {}

        def one_pass(name, blk, a, t, start, stop):
            ch = blk * BLOCK // CHUNK
            cols = slice(blk * BLOCK % CHUNK, blk * BLOCK % CHUNK + BLOCK)
            entries = slice(blk * BLOCK, (blk + 1) * BLOCK)
            plane = picked_sc[name][:, entries] if a == 0 else second_plane[name][:].bitcast(U8)[:, entries]
            lhsT, lhsT_scale = stationary(name, a, t)
            nc.tensor.matmul_mx(out=accumulators[name, blk][:, t, :], lhsT=lhsT, lhsT_scale=lhsT_scale,
                                rhs=picked_w[name, a, ch][:, cols].bitcast(FP8X4), rhs_scale=plane, start=start, stop=stop)

        def multiply(name, blk, bank):
            accumulators[name, blk] = take_bank(bank, [SLOTS, BLOCK])
            for t in range(SLOTS):
                for a in range(PASSES):
                    one_pass(name, blk, a, t, a == 0, a == PASSES - 1)
            sums[name, blk] = accumulators[name, blk][:].rearrange("p t j -> p j t")

        def multiply_pass(name, blk, bank, a):
            if a == 0:
                accumulators[name, blk] = take_bank(bank, [SLOTS, BLOCK])
            for t in range(SLOTS):
                one_pass(name, blk, a, t, a == 0 and t == 0, a == PASSES - 1 and t == SLOTS - 1)
            sums[name, blk] = accumulators[name, blk][:].rearrange("p t j -> p j t")

        def woven(ap):
            return ap.rearrange("p (j t) -> p j t", t=SLOTS)

        squares = [keep.tile([P, 2, H], F32, name="squares%d" % pair) for pair in range(BLOCKS // 2)]
        roots = [keep.tile([P, 2, H], F32, name="roots%d" % pair) for pair in range(BLOCKS // 2)]
        rates = {group: reused.tile([P, 2, H], BF16, name="rates%d" % group[0], offset=at, align_bytes=64)[:] for group, at in RATES_AT.items()}
        for blk in (6, 7):
            rates[(blk,)] = keep.tile([P, 1, H], BF16, name="rates%d" % blk, align_bytes=64)[:]
        damp = {}
        levels = {}
        damped = {}
        h_mx = {}

        def square_inhibitor(blk):
            nc.scalar.activation(woven(squares[blk // 2][:, blk % 2, :]), sums["i", blk], ACT.Square)

        def inverse_root(first, count=2):
            part = slice(first % 2, first % 2 + count)
            nc.scalar.activation(roots[first // 2][:, part, :], squares[first // 2][:, part, :], ACT.Abs_reciprocal_sqrt, bias=1.0)

        def damping(first, count=2):
            into = keep.tile([P, count, H], F32, name="damp%d" % first)
            nc.scalar.activation(into[:], roots[first // 2][:, first % 2 : first % 2 + count, :], ACT.Square)
            for g in range(count):
                damp[first + g] = into[:, g, :]

        def placed(name, shape, dtype, at):
            if at is None:
                return keep.tile([P] + shape, dtype, name=name, align_bytes=64)
            return reused.tile([P] + shape, dtype, name=name, offset=at, align_bytes=64)

        def copy_substrate(blk):
            levels[blk] = placed("level%d" % blk, [H], F32, LEVELS_AT.get(blk))
            nc.scalar.copy(woven(levels[blk][:]), sums["c", blk])

        def damp_substrate(blk):
            damped[blk] = placed("damped%d" % blk, [H], F32, DAMPED_AT.get(blk))[:]
            if blk in levels:
                nc.gpsimd.tensor_tensor(damped[blk], levels[blk][:], damp[blk], MULT)
            else:
                nc.vector.tensor_tensor(woven(damped[blk]), woven(damp[blk]), sums["c", blk], MULT)

        def rate(blk):
            group = [g for g in rates if blk in g][0]
            nc.vector.tensor_tensor(woven(rates[group][:, blk - group[0], :]), woven(damped[blk]), sums["e", blk], MULT)

        def quantise_rates(group):
            width = len(group) * BLOCK
            h_w = keep.tile([P, width], U32, name="h_w%d" % group[0], align_bytes=64)
            h_sc = keep.tile([P, width], U8, name="h_sc%d" % group[0], align_bytes=64)
            nc.vector.quantize_mx(out=h_w[:].bitcast(FP8X4), scales=h_sc[:], in_=rates[group].rearrange("p g x -> p (g x)"))
            h_mx[group] = h_w, h_sc

        def flux(group, first, bank, on_vector=False, count=2):
            h_w, h_sc = h_mx[group]
            width = len(group) * BLOCK
            st_bytes = st_w[:].bitcast(U8)
            st_plane = st_sc[:].bitcast(U8)
            result = keep.tile([P, count, width], F32, name="result%d_%d" % (group[0], first))
            y = take_bank(bank, [count, width])
            for c in range(first, first + count):
                nc.tensor.matmul_mx(out=y[:, c - first, :], lhsT=st_bytes[:, 2 * P * c : 2 * P * (c + 1)].bitcast(FP4X4),
                                    lhsT_scale=st_plane[:, P * c : P * (c + 1)],
                                    rhs=h_w[:].bitcast(FP8X4), rhs_scale=h_sc[:], start=True, stop=True)
            if on_vector:
                spread = bias[:, first : first + 2].unsqueeze(2).to_broadcast([P, 2, width])
                nc.vector.tensor_tensor(result[:], spread, y[:], ADD)
            else:
                for c in range(first, first + count):
                    nc.scalar.activation(result[:, c - first, :], y[:, c - first, :], ACT.Identity, bias=bias[:, c : c + 1])
            rows = out[first * P : (first + count) * P, group[0] * BLOCK : group[0] * BLOCK + width]
            nc.sync.dma_start(rows.rearrange("(c p) j -> p c j", p=P), result[:])

        nc.gpsimd.tensor_copy(wi_dealt[:].rearrange("p t (g i) -> p g t i", i=4),
                              wi_w[:].rearrange("p a (g i t) -> p (a g) t i", i=4, t=SLOTS))
        deal_plane(wi_sc_dealt, wi_sc)
        nc.gpsimd.tensor_copy(ws_dealt[:], ws_w[:].rearrange("p a y -> p (a y)").bitcast(U8).rearrange("p (m t h) -> p t m h", t=SLOTS, h=2))
        deal_plane(ws_sc_dealt, ws_sc)
        gather_words("i", 0, (0, 1))
        gather_words("c", 0, (0, 1))
        for blk in range(4):
            multiply_pass("i", blk, blk, 0)
        gather_words("i", 1, (0,))
        for blk in range(4):
            multiply_pass("i", blk, blk, 1)
        gather_words("c", 1, (0, 1))
        gather_words("i", 1, (1,))
        gather_scales("e")
        move_plane("e")
        gather_words("e", 0, (0, 1))
        gather_words("e", 1, (0,))
        for part in range(4):
            round_we(part)
        for blk in range(4):
            multiply("c", blk, 4 + blk)
        square_inhibitor(0)
        square_inhibitor(1)
        square_inhibitor(2)
        inverse_root(0)
        square_inhibitor(3)
        damping(0)
        copy_substrate(0)
        inverse_root(2)
        copy_substrate(1)
        damp_substrate(0)
        damp_substrate(1)
        nc.vector.quantize_mx(out=we_w[:].rearrange("p a t m -> p (a t m)").bitcast(FP8X4),
                              scales=we_sc[:].rearrange("p a t m -> p (a t m)"),
                              in_=we_bf[:].rearrange("p a t m j -> p (a t m j)"))
        late_words = reused.tile([P, CHUNK], U32, offset=LATE_WORDS_AT, align_bytes=64)
        gather_words("e", 1, (1,), late_words[:])

        multiply("i", 4, 4)
        multiply("i", 5, 5)
        for blk in range(4, BLOCKS):
            multiply("c", blk, blk - 4)
        damping(2)
        copy_substrate(2)
        multiply("i", 6, 6)
        damp_substrate(2)
        damp_substrate(3)
        for blk in (4, 5, 6):
            square_inhibitor(blk)
            multiply("e", blk - 4, blk)
        multiply("i", 7, 7)
        inverse_root(4)
        inverse_root(6, count=1)
        damping(4)
        square_inhibitor(7)
        damping(6, count=1)
        inverse_root(7, count=1)

        damp_substrate(4)
        rate(0)
        multiply("e", 3, 4)
        rate(1)
        multiply("e", 4, 5)
        rate(2)
        quantise_rates((0, 1))
        flux((0, 1), 0, 6)
        damping(7, count=1)
        multiply("e", 5, 0)
        rate(3)
        flux((0, 1), 2, 4)
        multiply("e", 7, 7)
        damp_substrate(5)
        multiply("e", 6, 1)
        quantise_rates((2, 3))
        flux((2, 3), 0, 6)
        flux((2, 3), 2, 4)
        rate(4)
        damp_substrate(6)
        rate(5)
        rate(6)
        quantise_rates((4, 5))
        flux((4, 5), 0, 5)
        flux((4, 5), 2, 0)
        damp_substrate(7)
        quantise_rates((6,))
        flux((6,), 0, 2)
        flux((6,), 2, 1)
        rate(7)
        quantise_rates((7,))
        flux((7,), 0, 3)
        flux((7,), 2, 7, on_vector=True)
